import numpy as np
import ml_dtypes


def mxq(x, axis, fmt="e4m3"):
    dtype, down = {"e4m3": (ml_dtypes.float8_e4m3fn, 7), "e5m2": (ml_dtypes.float8_e5m2, 14)}[fmt]
    v = np.moveaxis(np.asarray(x, np.float32).astype(ml_dtypes.bfloat16).astype(np.float64), axis, -1)
    blocks = v.reshape(v.shape[:-1] + (-1, 32))
    amax = np.abs(blocks).max(-1, keepdims=True)
    byte = np.maximum(np.where(amax > 0, np.frexp(amax)[1] - 1 + 127, 0) - down, 1)
    scale = np.exp2(byte - 127.0)
    codes = (blocks / scale).astype(np.float32).astype(dtype).astype(np.float64)
    return np.moveaxis((codes * scale).reshape(v.shape), -1, axis)


WIDE = False


def mx_kscale(k):
    if not WIDE:
        return np.ones(k)
    levels = np.array([10, -10, 5, -5, 0])
    if k % 512:
        return np.exp2(np.random.permutation(np.resize(levels, k // 32))).repeat(32)
    a = np.empty((k // 512, 16))
    for p in range(k // 512):
        a[p, :8] = np.random.permutation(np.resize(levels, 8))
        for g in range(8):
            far = levels[np.abs(levels - a[p, g]) >= 10]
            a[p, g + 8] = far[np.random.randint(len(far))]
    return np.exp2(a.ravel()).repeat(32)


def f64(x):
    return np.asarray(x).astype(np.float64)


def striped(idx):
    return np.tile(np.asarray(idx).reshape(-1, 16).T, (8, 1)).astype(np.uint16)


def unstriped(offs):
    return offs[:16].T.reshape(-1).astype(np.int64)


E2M1 = np.array([0.0, 0.5, 1.0, 1.5, 2.0, 3.0, 4.0, 6.0, -0.0, -0.5, -1.0, -1.5, -2.0, -3.0, -4.0, -6.0])


def pack_weight(w, fmt):
    k, n = w.shape
    w = f64(np.asarray(w, np.float32).astype(ml_dtypes.bfloat16)).reshape(k // 32, 32, n)
    amax = np.abs(w).max(1)
    if fmt == "e4m3":
        byte = np.frexp(amax)[1] - 1 + 127 - 7
    else:
        mant, ex = np.frexp(amax / 6.0)
        byte = np.where(mant > 0.5, ex, ex - 1) + 127
    byte = np.clip(np.where(amax > 0, byte, 1), 1, 254)
    scaled = (w * np.exp2(127.0 - byte)[:, None, :]).reshape(k, n).astype(np.float32)
    by_word = np.ascontiguousarray(scaled.reshape(k // 512, 128, 4, n).transpose(0, 1, 3, 2))
    if fmt == "e4m3":
        words = by_word.astype(ml_dtypes.float8_e4m3fn).view(np.uint8)
    else:
        c = by_word.astype(ml_dtypes.float4_e2m1fn).view(np.uint8) & 0xF
        words = (c[..., 0::2] | (c[..., 1::2] << 4)).reshape(k // 512, 128, 2 * n)
    return np.ascontiguousarray(words), np.ascontiguousarray(byte.astype(np.uint8).reshape(k // 512, 16, n))


def unpack_weight(words, scales, fmt):
    g, _, n = scales.shape
    words = np.ascontiguousarray(words).reshape(g, 128, n, -1)
    if fmt == "e4m3":
        vals = words.view(ml_dtypes.float8_e4m3fn).astype(np.float64)
    else:
        nib = np.empty((g, 128, n, 4), np.uint8)
        nib[..., 0::2] = words & 0xF
        nib[..., 1::2] = words >> 4
        vals = E2M1[nib]
    vals = vals * np.repeat(np.exp2(scales.astype(np.float64) - 127.0), 8, axis=1)[..., None]
    return vals.transpose(0, 1, 3, 2).reshape(g * 512, n)


def sigmoid(v):
    return 1.0 / (1.0 + np.exp(-v))


def bf(x):
    return np.asarray(x, np.float32).astype(ml_dtypes.bfloat16)


def planes(Y):
    r, m = Y.shape
    b = f64(bf(Y)).reshape(r // 32, 32, m)
    amax = np.abs(b).max(1)
    byte = np.clip(np.where(amax > 0, np.frexp(amax)[1] - 1 + 127 - 7, 1), 1, 254)
    codes = (b * np.exp2(127.0 - byte)[:, None, :]).reshape(r, m).astype(np.float32).astype(ml_dtypes.float8_e4m3fn).view(np.uint8)
    words = codes.reshape(r // 512, 128, 4, m).transpose(0, 1, 3, 2)
    return np.ascontiguousarray(words), np.ascontiguousarray(byte.astype(np.uint8).reshape(r // 512, 16, m))


B, N, T, D, NQ = 1, 512, 2048, 512, 512


def setup_inputs():
    n = np.random.standard_normal
    idx = np.random.permutation(T)[:B * N]
    s = mx_kscale(D)[:, None]
    kp = pack_weight(n((D, T)) / s, "e4m3")
    return {
        "qT": (n((B, D, NQ)) * s * (1.00 / np.sqrt(D))).astype(np.float32),
        "k_words": kp[0],
        "k_scales": kp[1],
        "ts": np.tile(np.random.uniform(0.5, 2.0, 2048), (128, 1)).astype(np.float32),
        "kb": np.tile(n(2048), (128, 1)).astype(np.float32),
        "offs": striped(idx),
    }


def reference(qT, k_words, k_scales, ts, kb, offs):
    idx = unstriped(offs)
    pick = lambda x, which: x[:, which].reshape(x.shape[0], B, -1).transpose(1, 0, 2)
    k = unpack_weight(k_words, k_scales, "e4m3")
    kg = pick(k, idx)
    qq = mxq(f64(qT), 1, "e4m3")
    a = qq.transpose(0, 2, 1) @ kg
    y = sigmoid(a * pick(f64(ts), idx)[:, :1, :] + pick(f64(kb), idx)[:, :1, :])
    Y = y[0]
    words, scales = planes(Y)
    return Y, words, scales

@@ -1,0 +1,159 @@
+from contextlib import ExitStack
+
+import concourse.mybir as mybir
+from concourse.masks import make_identity
+
+F32 = mybir.dt.float32
+BF16 = mybir.dt.bfloat16
+I32 = mybir.dt.int32
+U32 = mybir.dt.uint32
+U16 = mybir.dt.uint16
+U8 = mybir.dt.uint8
+FP8X4 = mybir.dt.float8_e4m3fn_x4
+SIGMOID = mybir.ActivationFunctionType.Sigmoid
+
+P = 128
+PACK = 4
+D, NQ, SLOTS, TOKENS = 512, 512, 512, 2048
+TILES = SLOTS // P
+HALF = 256
+FLOPS = 2 * D * NQ * SLOTS
+BYTES = 4 * D * NQ + 4 * P * TOKENS + 16 * TOKENS + 2 * 4 * TOKENS + 2 * P * 32 + 4 * NQ * SLOTS + NQ * SLOTS + 16 * SLOTS
+
+
+def tile_attend_plq_sigts_topk_kernel(tc, qT, k_words, k_scales, ts, kb, offs, out_0, out_1, out_2):
+    nc = tc.nc
+    with ExitStack() as ctx:
+        keep = ctx.enter_context(tc.tile_pool(name="keep", bufs=1))
+        psum = ctx.enter_context(tc.psum_pool(name="psum", bufs=1))
+
+        offsets = keep.tile([P, SLOTS // 16], U16, name="offsets")
+        ts_pool = keep.tile([P, TOKENS], F32, name="ts_pool")
+        kb_pool = keep.tile([P, TOKENS], F32, name="kb_pool")
+        scale_pool = keep.tile([P, TOKENS], U8, name="scale_pool", align_bytes=64)
+        word_pool = keep.tile([P, TOKENS], U32, name="word_pool", align_bytes=64)
+        q_raw = [keep.tile([P, PACK, HALF], F32, name="q_raw%d" % h) for h in range(2)]
+
+        nc.vector.memset(scale_pool[:].bitcast(I32), 0)
+        nc.vector.memset(ts_pool[0 : P - 1, :], 0.0)
+        nc.vector.memset(kb_pool[0 : P - 1, :], 0.0)
+
+        q_rows = qT[0].rearrange("(p j) c -> p j c", j=PACK)
+        nc.sync.dma_start(offsets[:], offs)
+        nc.sync.dma_start(ts_pool[P - 1 : P, :], ts[0:1, :])
+        nc.scalar.dma_start(q_raw[0][:], q_rows[:, :, 0:HALF])
+        nc.sync.dma_start(kb_pool[P - 1 : P, :], kb[0:1, :])
+        nc.scalar.dma_start(q_raw[1][:], q_rows[:, :, HALF:NQ])
+        for quad in range(4):
+            nc.sync.dma_start(
+                scale_pool[32 * quad : 32 * quad + 4, :].bitcast(I32),
+                k_scales[0][4 * quad : 4 * quad + 4, :].bitcast(I32),
+            )
+        nc.sync.dma_start(word_pool[:].bitcast(I32), k_words[0].rearrange("p n t -> p (n t)").bitcast(I32))
+
+        ident = keep.tile([P, P], F32, name="ident")
+        make_identity(nc, ident[:])
+        warm = keep.tile([P, 1], F32, name="warm")
+        nc.scalar.activation(warm[:], ident[:, 0:1], SIGMOID)
+
+        ts_g = keep.tile([P, SLOTS], F32, name="ts_g")
+        kb_g = keep.tile([P, SLOTS], F32, name="kb_g")
+        k_sc = keep.tile([P, SLOTS], U8, name="k_sc", align_bytes=64)
+        nc.vector.tensor_copy(ts_g[:], ts_pool[:].indirect(offsets[:]))
+        nc.vector.tensor_copy(kb_g[:], kb_pool[:].indirect(offsets[:]))
+        nc.vector.tensor_copy(k_sc[:], scale_pool[:].indirect(offsets[:]))
+
+        cols = []
+        for n, rows in enumerate((ts_g, kb_g)):
+            bank = psum.tile([P, TILES, P], F32, name="turn%d" % (2 + n), tag="turn%d" % (2 + n))
+            for s in range(TILES):
+                nc.tensor.transpose(bank[:, s, :], rows[:, s * P : (s + 1) * P], ident[:])
+            col = keep.tile([P, TILES], F32, name="col%d" % n)
+            nc.scalar.copy(col[:], bank[:, :, P - 1])
+            cols.append(col)
+
+        q_codes = keep.tile([P, NQ], U32, name="q_codes", align_bytes=64)
+        q_sc = keep.tile([P, NQ], U8, name="q_sc", align_bytes=64)
+        for h in range(2):
+            q_bf = keep.tile([P, HALF * PACK], BF16, name="q_bf%d" % h, align_bytes=64)
+            nc.scalar.copy(
+                q_bf[:].rearrange("p (c i t) -> p c t i", i=4, t=PACK),
+                q_raw[h][:].rearrange("p t (c i) -> p c t i", i=4),
+            )
+            nc.vector.quantize_mx(
+                out=q_codes[:, h * HALF : (h + 1) * HALF].bitcast(FP8X4),
+                scales=q_sc[:, h * HALF : (h + 1) * HALF],
+                in_=q_bf[:],
+            )
+
+        k_g = []
+        for h in range(2):
+            words = keep.tile([P, HALF], U32, name="k_g%d" % h, align_bytes=64)
+            nc.vector.tensor_copy(words[:], word_pool[:].indirect(offsets[:, 16 * h : 16 * (h + 1)]))
+            k_g.append(words)
+
+        y_codes = keep.tile([P, SLOTS], U32, name="y_codes", align_bytes=64)
+        y_sc = keep.tile([P, SLOTS], U8, name="y_sc", align_bytes=64)
+        out_rows = out_0.rearrange("(p t) i -> p t i", t=PACK)
+        out_words = out_1[0].rearrange("p i u -> p (i u)").bitcast(I32)
+
+        yT = {}
+
+        def score(s):
+            bank = psum.tile([P, NQ], F32, name="score%d" % s)
+            nc.tensor.matmul_mx(
+                out=bank[:],
+                lhsT=k_g[s // 2][:, (s % 2) * P : (s % 2 + 1) * P].bitcast(FP8X4),
+                lhsT_scale=k_sc[:, s * P : (s + 1) * P],
+                rhs=q_codes[:].bitcast(FP8X4),
+                rhs_scale=q_sc[:],
+                start=True,
+                stop=True,
+            )
+            yT[s] = keep.tile([P, PACK, P], F32, name="yT%d" % s)
+            nc.scalar.activation(
+                yT[s][:],
+                bank[:].rearrange("p (m t) -> p t m", t=PACK),
+                SIGMOID,
+                bias=cols[1][:, s : s + 1],
+                scale=cols[0][:, s : s + 1],
+            )
+
+        def finish(s):
+            bank = psum.tile([P, PACK, P], F32, name="turn%d" % s, tag="turn%d" % s)
+            for t in range(PACK):
+                nc.tensor.transpose(bank[:, t, :], yT[s][:, t, :], ident[:])
+            y = keep.tile([P, PACK, P], F32, name="y%d" % s)
+            if s < 2:
+                nc.vector.tensor_copy(y[:], bank[:])
+            else:
+                nc.scalar.copy(y[:], bank[:])
+            nc.sync.dma_start(out_rows[:, :, s * P : (s + 1) * P], y[:])
+            y_bf = keep.tile([P, P * PACK], BF16, name="y_bf%d" % s, align_bytes=64)
+            nc.vector.tensor_copy(
+                y_bf[:].rearrange("p (c i t) -> p c t i", i=4, t=PACK),
+                y[:].rearrange("p t (c i) -> p c t i", i=4),
+            )
+            nc.vector.quantize_mx(
+                out=y_codes[:, s * P : (s + 1) * P].bitcast(FP8X4),
+                scales=y_sc[:, s * P : (s + 1) * P],
+                in_=y_bf[:],
+            )
+            if s % 2 == 1:
+                half = slice((s - 1) * P, (s + 1) * P)
+                nc.sync.dma_start(out_words[:, half], y_codes[:, half].bitcast(I32))
+
+        score(0)
+        score(1)
+        finish(0)
+        score(2)
+        finish(1)
+        score(3)
+        finish(2)
+        finish(3)
+        for quad in range(4):
+            queue = nc.scalar if quad % 2 == 0 else nc.sync
+            queue.dma_start(
+                out_2[0][4 * quad : 4 * quad + 4, :].bitcast(I32),
+                y_sc[32 * quad : 32 * quad + 4, :].bitcast(I32),
+            )

@@ -32,18 +32,21 @@ def tile_attend_plq_sigts_topk_kernel(tc, qT, k_words, k_scales, ts, kb, offs, o
         kb_pool = keep.tile([P, TOKENS], F32, name="kb_pool")
         scale_pool = keep.tile([P, TOKENS], U8, name="scale_pool", align_bytes=64)
         word_pool = keep.tile([P, TOKENS], U32, name="word_pool", align_bytes=64)
-        q_raw = [keep.tile([P, PACK, HALF], F32, name="q_raw%d" % h) for h in range(2)]
+        q_raw = [keep.tile([P, PACK, HALF], F32, name="q_raw%d" % h, tag="q_raw%d" % h) for h in range(2)]
 
-        nc.vector.memset(scale_pool[:].bitcast(I32), 0)
-        nc.vector.memset(ts_pool[0 : P - 1, :], 0.0)
-        nc.vector.memset(kb_pool[0 : P - 1, :], 0.0)
+        nc.gpsimd.memset(scale_pool[:].bitcast(I32), 0)
+        nc.vector.memset(ts_pool[0 : P - 1, 0:1023], 0.0)
+        nc.vector.memset(ts_pool[0 : P - 1, 1023:TOKENS], 0.0)
+        ident = keep.tile([P, P], F32, name="ident")
+        make_identity(nc, ident[:])
+        nc.gpsimd.memset(kb_pool[0 : P - 1, :], 0.0)
 
         q_rows = qT[0].rearrange("(p j) c -> p j c", j=PACK)
         nc.sync.dma_start(offsets[:], offs)
         nc.sync.dma_start(ts_pool[P - 1 : P, :], ts[0:1, :])
-        nc.scalar.dma_start(q_raw[0][:], q_rows[:, :, 0:HALF])
         nc.sync.dma_start(kb_pool[P - 1 : P, :], kb[0:1, :])
-        nc.scalar.dma_start(q_raw[1][:], q_rows[:, :, HALF:NQ])
+        nc.sync.dma_start(q_raw[0][:], q_rows[:, :, 0:HALF])
+        nc.sync.dma_start(q_raw[1][:], q_rows[:, :, HALF:NQ])
         for quad in range(4):
             nc.sync.dma_start(
                 scale_pool[32 * quad : 32 * quad + 4, :].bitcast(I32),
@@ -51,26 +54,16 @@ def tile_attend_plq_sigts_topk_kernel(tc, qT, k_words, k_scales, ts, kb, offs, o
             )
         nc.sync.dma_start(word_pool[:].bitcast(I32), k_words[0].rearrange("p n t -> p (n t)").bitcast(I32))
 
-        ident = keep.tile([P, P], F32, name="ident")
-        make_identity(nc, ident[:])
         warm = keep.tile([P, 1], F32, name="warm")
-        nc.scalar.activation(warm[:], ident[:, 0:1], SIGMOID)
+        nc.vector.memset(warm[:], 0.0)
+        nc.scalar.activation(warm[:], warm[:], SIGMOID)
 
         ts_g = keep.tile([P, SLOTS], F32, name="ts_g")
         kb_g = keep.tile([P, SLOTS], F32, name="kb_g")
-        k_sc = keep.tile([P, SLOTS], U8, name="k_sc", align_bytes=64)
+        k_sc = [keep.tile([P, HALF], U8, name="k_sc%d" % h, align_bytes=64) for h in range(2)]
         nc.vector.tensor_copy(ts_g[:], ts_pool[:].indirect(offsets[:]))
         nc.vector.tensor_copy(kb_g[:], kb_pool[:].indirect(offsets[:]))
-        nc.vector.tensor_copy(k_sc[:], scale_pool[:].indirect(offsets[:]))
-
-        cols = []
-        for n, rows in enumerate((ts_g, kb_g)):
-            bank = psum.tile([P, TILES, P], F32, name="turn%d" % (2 + n), tag="turn%d" % (2 + n))
-            for s in range(TILES):
-                nc.tensor.transpose(bank[:, s, :], rows[:, s * P : (s + 1) * P], ident[:])
-            col = keep.tile([P, TILES], F32, name="col%d" % n)
-            nc.scalar.copy(col[:], bank[:, :, P - 1])
-            cols.append(col)
+        nc.vector.tensor_copy(k_sc[0][:], scale_pool[:].indirect(offsets[:, 0:16]))
 
         q_codes = keep.tile([P, NQ], U32, name="q_codes", align_bytes=64)
         q_sc = keep.tile([P, NQ], U8, name="q_sc", align_bytes=64)
@@ -86,11 +79,24 @@ def tile_attend_plq_sigts_topk_kernel(tc, qT, k_words, k_scales, ts, kb, offs, o
                 in_=q_bf[:],
             )
 
+        banks = []
+        for n, rows in enumerate((ts_g, kb_g)):
+            bank = psum.tile([P, TILES, P], F32, name="turn%d" % (2 + n), tag="turn%d" % (2 + n))
+            for s in range(TILES):
+                nc.tensor.transpose(bank[:, s, :], rows[:, s * P : (s + 1) * P], ident[:])
+            banks.append(bank)
+        col = keep.tile([P, 2, TILES], F32, name="col", tag="q_raw1")
+        cols = [col[:, 0, :], col[:, 1, :]]
+        for n in range(2):
+            nc.scalar.copy(cols[n], banks[n][:, :, P - 1])
+
         k_g = []
         for h in range(2):
             words = keep.tile([P, HALF], U32, name="k_g%d" % h, align_bytes=64)
             nc.vector.tensor_copy(words[:], word_pool[:].indirect(offsets[:, 16 * h : 16 * (h + 1)]))
             k_g.append(words)
+            if h == 0:
+                nc.vector.tensor_copy(k_sc[1][:], scale_pool[:].indirect(offsets[:, 16:32]))
 
         y_codes = keep.tile([P, SLOTS], U32, name="y_codes", align_bytes=64)
         y_sc = keep.tile([P, SLOTS], U8, name="y_sc", align_bytes=64)
@@ -104,7 +110,7 @@ def tile_attend_plq_sigts_topk_kernel(tc, qT, k_words, k_scales, ts, kb, offs, o
             nc.tensor.matmul_mx(
                 out=bank[:],
                 lhsT=k_g[s // 2][:, (s % 2) * P : (s % 2 + 1) * P].bitcast(FP8X4),
-                lhsT_scale=k_sc[:, s * P : (s + 1) * P],
+                lhsT_scale=k_sc[s // 2][:, (s % 2) * P : (s % 2 + 1) * P],
                 rhs=q_codes[:].bitcast(FP8X4),
                 rhs_scale=q_sc[:],
                 start=True,
@@ -119,38 +125,43 @@ def tile_attend_plq_sigts_topk_kernel(tc, qT, k_words, k_scales, ts, kb, offs, o
                 scale=cols[0][:, s : s + 1],
             )
 
-        def finish(s):
+        y = {}
+        y_bf = [keep.tile([P, HALF * PACK], BF16, name="y_bf%d" % h, align_bytes=64) for h in range(2)]
+
+        def turn(s):
             bank = psum.tile([P, PACK, P], F32, name="turn%d" % s, tag="turn%d" % s)
             for t in range(PACK):
                 nc.tensor.transpose(bank[:, t, :], yT[s][:, t, :], ident[:])
-            y = keep.tile([P, PACK, P], F32, name="y%d" % s)
-            if s < 2:
-                nc.vector.tensor_copy(y[:], bank[:])
+            y[s] = keep.tile([P, PACK, P], F32, name="y%d" % s)
+            if s in (0, 2):
+                nc.vector.tensor_copy(y[s][:], bank[:])
             else:
-                nc.scalar.copy(y[:], bank[:])
-            nc.sync.dma_start(out_rows[:, :, s * P : (s + 1) * P], y[:])
-            y_bf = keep.tile([P, P * PACK], BF16, name="y_bf%d" % s, align_bytes=64)
-            nc.vector.tensor_copy(
-                y_bf[:].rearrange("p (c i t) -> p c t i", i=4, t=PACK),
-                y[:].rearrange("p t (c i) -> p c t i", i=4),
-            )
-            nc.vector.quantize_mx(
-                out=y_codes[:, s * P : (s + 1) * P].bitcast(FP8X4),
-                scales=y_sc[:, s * P : (s + 1) * P],
-                in_=y_bf[:],
-            )
-            if s % 2 == 1:
-                half = slice((s - 1) * P, (s + 1) * P)
-                nc.sync.dma_start(out_words[:, half], y_codes[:, half].bitcast(I32))
+                nc.scalar.copy(y[s][:], bank[:])
+            nc.sync.dma_start(out_rows[:, :, s * P : (s + 1) * P], y[s][:])
 
-        score(0)
-        score(1)
-        finish(0)
-        score(2)
-        finish(1)
-        score(3)
-        finish(2)
-        finish(3)
+        def weave(s):
+            dst = y_bf[s // 2][:, (s % 2) * P * PACK : (s % 2 + 1) * P * PACK].rearrange("p (c i t) -> p c t i", i=4, t=PACK)
+            src = y[s][:].rearrange("p t (c i) -> p c t i", i=4)
+            if s in (0, 1, 2):
+                nc.vector.tensor_copy(dst, src)
+            else:
+                nc.scalar.copy(dst, src)
+
+        def quantize(h):
+            half = slice(h * HALF, (h + 1) * HALF)
+            nc.vector.quantize_mx(out=y_codes[:, half].bitcast(FP8X4), scales=y_sc[:, half], in_=y_bf[h][:])
+            nc.sync.dma_start(out_words[:, half], y_codes[:, half].bitcast(I32))
+
+        for s in range(TILES):
+            score(s)
+        for s in range(TILES):
+            turn(s)
+        weave(0)
+        weave(1)
+        weave(2)
+        quantize(0)
+        weave(3)
+        quantize(1)
         for quad in range(4):
             queue = nc.scalar if quad % 2 == 0 else nc.sync
             queue.dma_start(

@@ -90,6 +90,17 @@ def tile_attend_plq_sigts_topk_kernel(tc, qT, k_words, k_scales, ts, kb, offs, o
         for n in range(2):
             nc.scalar.copy(cols[n], banks[n][:, :, P - 1])
 
+        spare = psum.tile([P, NQ], F32, name="spare", tag="turn1")
+        nc.tensor.matmul_mx(
+            out=spare[:],
+            lhsT=q_codes[:, 0:P].bitcast(FP8X4),
+            lhsT_scale=q_sc[:, 0:P],
+            rhs=q_codes[:].bitcast(FP8X4),
+            rhs_scale=q_sc[:],
+            start=True,
+            stop=True,
+        )
+
         k_g = []
         for h in range(2):
             words = keep.tile([P, HALF], U32, name="k_g%d" % h, align_bytes=64)
@@ -125,23 +136,28 @@ def tile_attend_plq_sigts_topk_kernel(tc, qT, k_words, k_scales, ts, kb, offs, o
                 scale=cols[0][:, s : s + 1],
             )
 
-        y = {}
+        y_0 = keep.tile([P, PACK, P], F32, name="y_0")
+        y_1 = keep.tile([P, PACK, P], F32, name="y_1")
+        y_last = keep.tile([P, PACK, HALF], F32, name="y_last")
+        y = [y_0[:], y_1[:], y_last[:, :, 0:P], y_last[:, :, P:HALF]]
         y_bf = [keep.tile([P, HALF * PACK], BF16, name="y_bf%d" % h, align_bytes=64) for h in range(2)]
 
         def turn(s):
             bank = psum.tile([P, PACK, P], F32, name="turn%d" % s, tag="turn%d" % s)
             for t in range(PACK):
                 nc.tensor.transpose(bank[:, t, :], yT[s][:, t, :], ident[:])
-            y[s] = keep.tile([P, PACK, P], F32, name="y%d" % s)
             if s in (0, 2):
-                nc.vector.tensor_copy(y[s][:], bank[:])
+                nc.vector.tensor_copy(y[s], bank[:])
             else:
-                nc.scalar.copy(y[s][:], bank[:])
-            nc.sync.dma_start(out_rows[:, :, s * P : (s + 1) * P], y[s][:])
+                nc.scalar.copy(y[s], bank[:])
+            if s < 2:
+                nc.sync.dma_start(out_rows[:, :, s * P : (s + 1) * P], y[s])
+            if s == 3:
+                nc.sync.dma_start(out_rows[:, :, HALF:SLOTS], y_last[:])
 
         def weave(s):
             dst = y_bf[s // 2][:, (s % 2) * P * PACK : (s % 2 + 1) * P * PACK].rearrange("p (c i t) -> p c t i", i=4, t=PACK)
-            src = y[s][:].rearrange("p t (c i) -> p c t i", i=4)
+            src = y[s].rearrange("p t (c i) -> p c t i", i=4)
             if s in (0, 1, 2):
                 nc.vector.tensor_copy(dst, src)
             else:

@@ -30,9 +30,9 @@ def tile_attend_plq_sigts_topk_kernel(tc, qT, k_words, k_scales, ts, kb, offs, o
         offsets = keep.tile([P, SLOTS // 16], U16, name="offsets")
         ts_pool = keep.tile([P, TOKENS], F32, name="ts_pool")
         kb_pool = keep.tile([P, TOKENS], F32, name="kb_pool")
-        scale_pool = keep.tile([P, TOKENS], U8, name="scale_pool", align_bytes=64)
+        scale_pool = keep.tile([P, TOKENS], U8, name="scale_pool", tag="scale_pool", align_bytes=64)
         word_pool = keep.tile([P, TOKENS], U32, name="word_pool", align_bytes=64)
-        q_raw = [keep.tile([P, PACK, HALF], F32, name="q_raw%d" % h, tag="q_raw%d" % h) for h in range(2)]
+        q_raw = keep.tile([P, PACK, NQ], F32, name="q_raw", tag="q_raw")
 
         nc.gpsimd.memset(scale_pool[:].bitcast(I32), 0)
         nc.vector.memset(ts_pool[0 : P - 1, 0:1023], 0.0)
@@ -45,8 +45,7 @@ def tile_attend_plq_sigts_topk_kernel(tc, qT, k_words, k_scales, ts, kb, offs, o
         nc.sync.dma_start(offsets[:], offs)
         nc.sync.dma_start(ts_pool[P - 1 : P, :], ts[0:1, :])
         nc.sync.dma_start(kb_pool[P - 1 : P, :], kb[0:1, :])
-        nc.sync.dma_start(q_raw[0][:], q_rows[:, :, 0:HALF])
-        nc.sync.dma_start(q_raw[1][:], q_rows[:, :, HALF:NQ])
+        nc.sync.dma_start(q_raw[:], q_rows)
         for quad in range(4):
             nc.sync.dma_start(
                 scale_pool[32 * quad : 32 * quad + 4, :].bitcast(I32),
@@ -60,19 +59,22 @@ def tile_attend_plq_sigts_topk_kernel(tc, qT, k_words, k_scales, ts, kb, offs, o
 
         ts_g = keep.tile([P, SLOTS], F32, name="ts_g")
         kb_g = keep.tile([P, SLOTS], F32, name="kb_g")
-        k_sc = [keep.tile([P, HALF], U8, name="k_sc%d" % h, align_bytes=64) for h in range(2)]
+        k_sc = keep.tile([P, SLOTS], U8, name="k_sc", align_bytes=64)
         nc.vector.tensor_copy(ts_g[:], ts_pool[:].indirect(offsets[:]))
         nc.vector.tensor_copy(kb_g[:], kb_pool[:].indirect(offsets[:]))
-        nc.vector.tensor_copy(k_sc[0][:], scale_pool[:].indirect(offsets[:, 0:16]))
+        nc.vector.tensor_copy(k_sc[:], scale_pool[:].indirect(offsets[:]))
 
-        q_codes = keep.tile([P, NQ], U32, name="q_codes", align_bytes=64)
+        q_codes = keep.tile([P, NQ], U32, name="q_codes", tag="scale_pool", align_bytes=64)
         q_sc = keep.tile([P, NQ], U8, name="q_sc", align_bytes=64)
         for h in range(2):
             q_bf = keep.tile([P, HALF * PACK], BF16, name="q_bf%d" % h, align_bytes=64)
-            nc.scalar.copy(
-                q_bf[:].rearrange("p (c i t) -> p c t i", i=4, t=PACK),
-                q_raw[h][:].rearrange("p t (c i) -> p c t i", i=4),
-            )
+            for lo, hi, on_vector in ((0, HALF, False),) if h == 0 else ((0, 128, False), (128, HALF, True)):
+                dst = q_bf[:, lo * PACK : hi * PACK].rearrange("p (c i t) -> p c t i", i=4, t=PACK)
+                src = q_raw[:, :, h * HALF + lo : h * HALF + hi].rearrange("p t (c i) -> p c t i", i=4)
+                if on_vector:
+                    nc.vector.tensor_copy(dst, src)
+                else:
+                    nc.scalar.copy(dst, src)
             nc.vector.quantize_mx(
                 out=q_codes[:, h * HALF : (h + 1) * HALF].bitcast(FP8X4),
                 scales=q_sc[:, h * HALF : (h + 1) * HALF],
@@ -85,7 +87,7 @@ def tile_attend_plq_sigts_topk_kernel(tc, qT, k_words, k_scales, ts, kb, offs, o
             for s in range(TILES):
                 nc.tensor.transpose(bank[:, s, :], rows[:, s * P : (s + 1) * P], ident[:])
             banks.append(bank)
-        col = keep.tile([P, 2, TILES], F32, name="col", tag="q_raw1")
+        col = keep.tile([P, 2, TILES], F32, name="col", tag="q_raw")
         cols = [col[:, 0, :], col[:, 1, :]]
         for n in range(2):
             nc.scalar.copy(cols[n], banks[n][:, :, P - 1])
@@ -106,8 +108,6 @@ def tile_attend_plq_sigts_topk_kernel(tc, qT, k_words, k_scales, ts, kb, offs, o
             words = keep.tile([P, HALF], U32, name="k_g%d" % h, align_bytes=64)
             nc.vector.tensor_copy(words[:], word_pool[:].indirect(offsets[:, 16 * h : 16 * (h + 1)]))
             k_g.append(words)
-            if h == 0:
-                nc.vector.tensor_copy(k_sc[1][:], scale_pool[:].indirect(offsets[:, 16:32]))
 
         y_codes = keep.tile([P, SLOTS], U32, name="y_codes", align_bytes=64)
         y_sc = keep.tile([P, SLOTS], U8, name="y_sc", align_bytes=64)
@@ -121,7 +121,7 @@ def tile_attend_plq_sigts_topk_kernel(tc, qT, k_words, k_scales, ts, kb, offs, o
             nc.tensor.matmul_mx(
                 out=bank[:],
                 lhsT=k_g[s // 2][:, (s % 2) * P : (s % 2 + 1) * P].bitcast(FP8X4),
-                lhsT_scale=k_sc[s // 2][:, (s % 2) * P : (s % 2 + 1) * P],
+                lhsT_scale=k_sc[:, s * P : (s + 1) * P],
                 rhs=q_codes[:].bitcast(FP8X4),
                 rhs_scale=q_sc[:],
                 start=True,

@@ -11,12 +11,16 @@ U16 = mybir.dt.uint16
 U8 = mybir.dt.uint8
 FP8X4 = mybir.dt.float8_e4m3fn_x4
 SIGMOID = mybir.ActivationFunctionType.Sigmoid
+MULT = mybir.AluOpType.mult
+ADD = mybir.AluOpType.add
 
 P = 128
 PACK = 4
 D, NQ, SLOTS, TOKENS = 512, 512, 512, 2048
 TILES = SLOTS // P
 HALF = 256
+EARLY = 384
+LATE = NQ - EARLY
 FLOPS = 2 * D * NQ * SLOTS
 BYTES = 4 * D * NQ + 4 * P * TOKENS + 16 * TOKENS + 2 * 4 * TOKENS + 2 * P * 32 + 4 * NQ * SLOTS + NQ * SLOTS + 16 * SLOTS
 
@@ -32,26 +36,29 @@ def tile_attend_plq_sigts_topk_kernel(tc, qT, k_words, k_scales, ts, kb, offs, o
         kb_pool = keep.tile([P, TOKENS], F32, name="kb_pool")
         scale_pool = keep.tile([P, TOKENS], U8, name="scale_pool", tag="scale_pool", align_bytes=64)
         word_pool = keep.tile([P, TOKENS], U32, name="word_pool", align_bytes=64)
-        q_raw = keep.tile([P, PACK, NQ], F32, name="q_raw", tag="q_raw")
+        q_early = keep.tile([P, PACK, EARLY], F32, name="q_early", tag="q_early")
+        q_late = keep.tile([P, PACK, LATE], F32, name="q_late")
 
         nc.gpsimd.memset(scale_pool[:].bitcast(I32), 0)
-        nc.vector.memset(ts_pool[0 : P - 1, 0:1023], 0.0)
-        nc.vector.memset(ts_pool[0 : P - 1, 1023:TOKENS], 0.0)
+        nc.vector.memset(ts_pool[0 : P - 1, 0:895], 0.0)
+        nc.vector.memset(ts_pool[0 : P - 1, 895:1792], 0.0)
+        nc.gpsimd.memset(ts_pool[0 : P - 1, 1792:TOKENS], 0.0)
+        nc.gpsimd.memset(kb_pool[0 : P - 1, :], 0.0)
         ident = keep.tile([P, P], F32, name="ident")
         make_identity(nc, ident[:])
-        nc.gpsimd.memset(kb_pool[0 : P - 1, :], 0.0)
 
         q_rows = qT[0].rearrange("(p j) c -> p j c", j=PACK)
         nc.sync.dma_start(offsets[:], offs)
         nc.sync.dma_start(ts_pool[P - 1 : P, :], ts[0:1, :])
         nc.sync.dma_start(kb_pool[P - 1 : P, :], kb[0:1, :])
-        nc.sync.dma_start(q_raw[:], q_rows)
+        nc.sync.dma_start(q_early[:], q_rows[:, :, 0:EARLY])
         for quad in range(4):
             nc.sync.dma_start(
                 scale_pool[32 * quad : 32 * quad + 4, :].bitcast(I32),
                 k_scales[0][4 * quad : 4 * quad + 4, :].bitcast(I32),
             )
         nc.sync.dma_start(word_pool[:].bitcast(I32), k_words[0].rearrange("p n t -> p (n t)").bitcast(I32))
+        nc.sync.dma_start(q_late[:], q_rows[:, :, EARLY:NQ])
 
         warm = keep.tile([P, 1], F32, name="warm")
         nc.vector.memset(warm[:], 0.0)
@@ -66,99 +73,112 @@ def tile_attend_plq_sigts_topk_kernel(tc, qT, k_words, k_scales, ts, kb, offs, o
 
         q_codes = keep.tile([P, NQ], U32, name="q_codes", tag="scale_pool", align_bytes=64)
         q_sc = keep.tile([P, NQ], U8, name="q_sc", align_bytes=64)
-        for h in range(2):
-            q_bf = keep.tile([P, HALF * PACK], BF16, name="q_bf%d" % h, align_bytes=64)
-            for lo, hi, on_vector in ((0, HALF, False),) if h == 0 else ((0, 128, False), (128, HALF, True)):
-                dst = q_bf[:, lo * PACK : hi * PACK].rearrange("p (c i t) -> p c t i", i=4, t=PACK)
-                src = q_raw[:, :, h * HALF + lo : h * HALF + hi].rearrange("p t (c i) -> p c t i", i=4)
-                if on_vector:
-                    nc.vector.tensor_copy(dst, src)
-                else:
-                    nc.scalar.copy(dst, src)
-            nc.vector.quantize_mx(
-                out=q_codes[:, h * HALF : (h + 1) * HALF].bitcast(FP8X4),
-                scales=q_sc[:, h * HALF : (h + 1) * HALF],
-                in_=q_bf[:],
+
+        def quantize_queries(raw, raw_lo, lo, hi):
+            q_bf = keep.tile([P, (hi - lo) * PACK], BF16, name="q_bf%d" % lo, tag="q_bf%d" % lo, align_bytes=64)
+            nc.scalar.copy(
+                q_bf[:].rearrange("p (c i t) -> p c t i", i=4, t=PACK),
+                raw[:, :, lo - raw_lo : hi - raw_lo].rearrange("p t (c i) -> p c t i", i=4),
             )
+            nc.vector.quantize_mx(out=q_codes[:, lo:hi].bitcast(FP8X4), scales=q_sc[:, lo:hi], in_=q_bf[:])
+
+        quantize_queries(q_early, 0, 0, HALF)
+        quantize_queries(q_early, 0, HALF, EARLY)
 
         banks = []
         for n, rows in enumerate((ts_g, kb_g)):
-            bank = psum.tile([P, TILES, P], F32, name="turn%d" % (2 + n), tag="turn%d" % (2 + n))
+            bank = psum.tile([P, TILES, P], F32, name="rows%d" % n, tag="turn%d" % n)
             for s in range(TILES):
                 nc.tensor.transpose(bank[:, s, :], rows[:, s * P : (s + 1) * P], ident[:])
             banks.append(bank)
-        col = keep.tile([P, 2, TILES], F32, name="col", tag="q_raw")
-        cols = [col[:, 0, :], col[:, 1, :]]
+        col = keep.tile([P, 2, TILES], F32, name="col", tag="q_early")
         for n in range(2):
-            nc.scalar.copy(cols[n], banks[n][:, :, P - 1])
+            nc.scalar.copy(col[:, n, :], banks[n][:, :, P - 1])
 
-        spare = psum.tile([P, NQ], F32, name="spare", tag="turn1")
-        nc.tensor.matmul_mx(
-            out=spare[:],
-            lhsT=q_codes[:, 0:P].bitcast(FP8X4),
-            lhsT_scale=q_sc[:, 0:P],
-            rhs=q_codes[:].bitcast(FP8X4),
-            rhs_scale=q_sc[:],
-            start=True,
-            stop=True,
-        )
+        spare = psum.tile([P, 2, HALF], F32, name="spare", tag="turn2")
+        for n in range(2):
+            nc.tensor.matmul_mx(
+                out=spare[:, n, :],
+                lhsT=q_codes[:, 0:P].bitcast(FP8X4),
+                lhsT_scale=q_sc[:, 0:P],
+                rhs=q_codes[:, 0:HALF].bitcast(FP8X4),
+                rhs_scale=q_sc[:, 0:HALF],
+                start=True,
+                stop=True,
+            )
 
         k_g = []
         for h in range(2):
             words = keep.tile([P, HALF], U32, name="k_g%d" % h, align_bytes=64)
             nc.vector.tensor_copy(words[:], word_pool[:].indirect(offsets[:, 16 * h : 16 * (h + 1)]))
             k_g.append(words)
+        quantize_queries(q_late, EARLY, EARLY, NQ)
 
         y_codes = keep.tile([P, SLOTS], U32, name="y_codes", align_bytes=64)
         y_sc = keep.tile([P, SLOTS], U8, name="y_sc", align_bytes=64)
         out_rows = out_0.rearrange("(p t) i -> p t i", t=PACK)
         out_words = out_1[0].rearrange("p i u -> p (i u)").bitcast(I32)
 
-        yT = {}
+        yT = [keep.tile([P, PACK, P], F32, name="yT%d" % s, align_bytes=64) for s in range(TILES)]
+        scores = [psum.tile([P, NQ], F32, name="score%d" % s, tag="score%d" % s) for s in range(TILES)]
 
-        def score(s):
-            bank = psum.tile([P, NQ], F32, name="score%d" % s)
+        late_scores = psum.tile([P, 2, LATE], F32, name="late_scores")
+
+        def bank_of(s, lo, hi):
+            return late_scores[:, s, :] if lo == EARLY else scores[s][:, lo:hi]
+
+        def product(s, lo, hi):
             nc.tensor.matmul_mx(
-                out=bank[:],
+                out=bank_of(s, lo, hi),
                 lhsT=k_g[s // 2][:, (s % 2) * P : (s % 2 + 1) * P].bitcast(FP8X4),
                 lhsT_scale=k_sc[:, s * P : (s + 1) * P],
-                rhs=q_codes[:].bitcast(FP8X4),
-                rhs_scale=q_sc[:],
+                rhs=q_codes[:, lo:hi].bitcast(FP8X4),
+                rhs_scale=q_sc[:, lo:hi],
                 start=True,
                 stop=True,
             )
-            yT[s] = keep.tile([P, PACK, P], F32, name="yT%d" % s)
+
+        def weigh(s, lo, hi):
             nc.scalar.activation(
-                yT[s][:],
-                bank[:].rearrange("p (m t) -> p t m", t=PACK),
+                yT[s][:, :, lo // PACK : hi // PACK],
+                bank_of(s, lo, hi).rearrange("p (m t) -> p t m", t=PACK),
                 SIGMOID,
-                bias=cols[1][:, s : s + 1],
-                scale=cols[0][:, s : s + 1],
+                bias=col[:, 1, s : s + 1],
+                scale=col[:, 0, s : s + 1],
             )
 
-        y_0 = keep.tile([P, PACK, P], F32, name="y_0")
-        y_1 = keep.tile([P, PACK, P], F32, name="y_1")
-        y_last = keep.tile([P, PACK, HALF], F32, name="y_last")
-        y = [y_0[:], y_1[:], y_last[:, :, 0:P], y_last[:, :, P:HALF]]
+        for s in range(2):
+            product(s, 0, HALF)
+            product(s, HALF, EARLY)
+            weigh(s, 0, EARLY)
+        for s in range(2):
+            product(s, EARLY, NQ)
+        for s in range(2):
+            weigh(s, EARLY, NQ)
+        for s in range(2, TILES):
+            product(s, 0, NQ)
+            weigh(s, 0, NQ)
+
+        y = [keep.tile([P, PACK, HALF], F32, name="y%d" % h) for h in range(2)]
         y_bf = [keep.tile([P, HALF * PACK], BF16, name="y_bf%d" % h, align_bytes=64) for h in range(2)]
 
-        def turn(s):
-            bank = psum.tile([P, PACK, P], F32, name="turn%d" % s, tag="turn%d" % s)
-            for t in range(PACK):
-                nc.tensor.transpose(bank[:, t, :], yT[s][:, t, :], ident[:])
-            if s in (0, 2):
-                nc.vector.tensor_copy(y[s], bank[:])
+        def turn(h, pair):
+            bank = psum.tile([P, 2, 2, P], F32, name="turn%d" % (2 * h + pair), tag=("turn0", "turn1", "turn2", "score0")[2 * h + pair])
+            for u in range(2):
+                for s in range(2):
+                    nc.tensor.transpose(bank[:, u, s, :], yT[2 * h + s][:, 2 * pair + u, :], ident[:])
+            rows = slice(2 * pair, 2 * pair + 2)
+            src = bank[:].rearrange("p u s i -> p u (s i)")
+            if pair == 0:
+                nc.vector.tensor_copy(y[h][:, rows, :], src)
             else:
-                nc.scalar.copy(y[s], bank[:])
-            if s < 2:
-                nc.sync.dma_start(out_rows[:, :, s * P : (s + 1) * P], y[s])
-            if s == 3:
-                nc.sync.dma_start(out_rows[:, :, HALF:SLOTS], y_last[:])
+                nc.scalar.copy(y[h][:, rows, :], src)
+            nc.sync.dma_start(out_rows[:, rows, h * HALF : (h + 1) * HALF], y[h][:, rows, :])
 
-        def weave(s):
-            dst = y_bf[s // 2][:, (s % 2) * P * PACK : (s % 2 + 1) * P * PACK].rearrange("p (c i t) -> p c t i", i=4, t=PACK)
-            src = y[s].rearrange("p t (c i) -> p c t i", i=4)
-            if s in (0, 1, 2):
+        def weave(h, lo, hi, on_vector):
+            dst = y_bf[h][:, lo * PACK : hi * PACK].rearrange("p (c i t) -> p c t i", i=4, t=PACK)
+            src = y[h][:, :, lo:hi].rearrange("p t (c i) -> p c t i", i=4)
+            if on_vector:
                 nc.vector.tensor_copy(dst, src)
             else:
                 nc.scalar.copy(dst, src)
@@ -168,15 +188,13 @@ def tile_attend_plq_sigts_topk_kernel(tc, qT, k_words, k_scales, ts, kb, offs, o
             nc.vector.quantize_mx(out=y_codes[:, half].bitcast(FP8X4), scales=y_sc[:, half], in_=y_bf[h][:])
             nc.sync.dma_start(out_words[:, half], y_codes[:, half].bitcast(I32))
 
-        for s in range(TILES):
-            score(s)
-        for s in range(TILES):
-            turn(s)
-        weave(0)
-        weave(1)
-        weave(2)
+        for h in range(2):
+            for pair in range(2):
+                turn(h, pair)
+        weave(0, 0, HALF, True)
+        weave(1, 0, 128, True)
+        weave(1, 128, HALF, False)
         quantize(0)
-        weave(3)
         quantize(1)
         for quad in range(4):
             queue = nc.scalar if quad % 2 == 0 else nc.sync

@@ -122,7 +122,7 @@ def tile_attend_plq_sigts_topk_kernel(tc, qT, k_words, k_scales, ts, kb, offs, o
         yT = [keep.tile([P, PACK, P], F32, name="yT%d" % s, align_bytes=64) for s in range(TILES)]
         scores = [psum.tile([P, NQ], F32, name="score%d" % s, tag="score%d" % s) for s in range(TILES)]
 
-        late_scores = psum.tile([P, 2, LATE], F32, name="late_scores")
+        late_scores = psum.tile([P, 2, LATE], F32, name="late_scores", tag="late")
 
         def bank_of(s, lo, hi):
             return late_scores[:, s, :] if lo == EARLY else scores[s][:, lo:hi]
@@ -162,24 +162,27 @@ def tile_attend_plq_sigts_topk_kernel(tc, qT, k_words, k_scales, ts, kb, offs, o
         y = [keep.tile([P, PACK, HALF], F32, name="y%d" % h) for h in range(2)]
         y_bf = [keep.tile([P, HALF * PACK], BF16, name="y_bf%d" % h, align_bytes=64) for h in range(2)]
 
-        def turn(h, pair):
-            bank = psum.tile([P, 2, 2, P], F32, name="turn%d" % (2 * h + pair), tag=("turn0", "turn1", "turn2", "score0")[2 * h + pair])
-            for u in range(2):
+        def turn(h, lo, hi, tag, on_vector):
+            bank = psum.tile([P, hi - lo, 2, P], F32, name="turned%d_%d" % (h, lo), tag=tag)
+            for t in range(lo, hi):
                 for s in range(2):
-                    nc.tensor.transpose(bank[:, u, s, :], yT[2 * h + s][:, 2 * pair + u, :], ident[:])
-            rows = slice(2 * pair, 2 * pair + 2)
+                    nc.tensor.transpose(bank[:, t - lo, s, :], yT[2 * h + s][:, t, :], ident[:])
             src = bank[:].rearrange("p u s i -> p u (s i)")
-            if pair == 0:
-                nc.vector.tensor_copy(y[h][:, rows, :], src)
+            if on_vector:
+                nc.vector.tensor_copy(y[h][:, lo:hi, :], src)
             else:
-                nc.scalar.copy(y[h][:, rows, :], src)
-            nc.sync.dma_start(out_rows[:, rows, h * HALF : (h + 1) * HALF], y[h][:, rows, :])
+                nc.scalar.copy(y[h][:, lo:hi, :], src)
 
-        def weave(h, lo, hi, on_vector):
+        def store(h, lo, hi):
+            nc.sync.dma_start(out_rows[:, lo:hi, h * HALF : (h + 1) * HALF], y[h][:, lo:hi, :])
+
+        def weave(h, lo, hi, engine):
             dst = y_bf[h][:, lo * PACK : hi * PACK].rearrange("p (c i t) -> p c t i", i=4, t=PACK)
             src = y[h][:, :, lo:hi].rearrange("p t (c i) -> p c t i", i=4)
-            if on_vector:
+            if engine == "v":
                 nc.vector.tensor_copy(dst, src)
+            elif engine == "g":
+                nc.gpsimd.tensor_copy(dst, src)
             else:
                 nc.scalar.copy(dst, src)
 
@@ -188,12 +191,28 @@ def tile_attend_plq_sigts_topk_kernel(tc, qT, k_words, k_scales, ts, kb, offs, o
             nc.vector.quantize_mx(out=y_codes[:, half].bitcast(FP8X4), scales=y_sc[:, half], in_=y_bf[h][:])
             nc.sync.dma_start(out_words[:, half], y_codes[:, half].bitcast(I32))
 
-        for h in range(2):
-            for pair in range(2):
-                turn(h, pair)
-        weave(0, 0, HALF, True)
-        weave(1, 0, 128, True)
-        weave(1, 128, HALF, False)
+        def turn_tile(s, lo, hi, tag, on_vector):
+            bank = psum.tile([P, hi - lo, P], F32, name="turned_tile%d_%d" % (s, lo), tag=tag)
+            for t in range(lo, hi):
+                nc.tensor.transpose(bank[:, t - lo, :], yT[s][:, t, :], ident[:])
+            dst = y[1][:, lo:hi, (s % 2) * P : (s % 2 + 1) * P]
+            if on_vector:
+                nc.vector.tensor_copy(dst, bank[:])
+            else:
+                nc.scalar.copy(dst, bank[:])
+
+        turn(0, 0, 1, "turn0", True)
+        store(0, 0, 1)
+        turn(0, 1, 2, "turn1", True)
+        store(0, 1, 2)
+        turn(0, 2, 4, "turn2", False)
+        store(0, 2, 4)
+        turn_tile(2, 0, 4, "score0", True)
+        turn_tile(3, 0, 4, "score1", False)
+        store(1, 0, 4)
+        weave(0, 0, HALF, "v")
+        weave(1, 0, 128, "v")
+        weave(1, 128, HALF, "s")
         quantize(0)
         quantize(1)
         for quad in range(4):

@@ -19,7 +19,7 @@ PACK = 4
 D, NQ, SLOTS, TOKENS = 512, 512, 512, 2048
 TILES = SLOTS // P
 HALF = 256
-EARLY = 384
+EARLY = 256
 LATE = NQ - EARLY
 FLOPS = 2 * D * NQ * SLOTS
 BYTES = 4 * D * NQ + 4 * P * TOKENS + 16 * TOKENS + 2 * 4 * TOKENS + 2 * P * 32 + 4 * NQ * SLOTS + NQ * SLOTS + 16 * SLOTS
@@ -37,7 +37,8 @@ def tile_attend_plq_sigts_topk_kernel(tc, qT, k_words, k_scales, ts, kb, offs, o
         scale_pool = keep.tile([P, TOKENS], U8, name="scale_pool", tag="scale_pool", align_bytes=64)
         word_pool = keep.tile([P, TOKENS], U32, name="word_pool", align_bytes=64)
         q_early = keep.tile([P, PACK, EARLY], F32, name="q_early", tag="q_early")
-        q_late = keep.tile([P, PACK, LATE], F32, name="q_late")
+        q_late_tile = keep.tile([P, 2, PACK, P], F32, name="q_late", tag="q_late", align_bytes=64)
+        q_late = [q_late_tile[:, n] for n in range(2)]
 
         nc.gpsimd.memset(scale_pool[:].bitcast(I32), 0)
         nc.vector.memset(ts_pool[0 : P - 1, 0:895], 0.0)
@@ -58,7 +59,8 @@ def tile_attend_plq_sigts_topk_kernel(tc, qT, k_words, k_scales, ts, kb, offs, o
                 k_scales[0][4 * quad : 4 * quad + 4, :].bitcast(I32),
             )
         nc.sync.dma_start(word_pool[:].bitcast(I32), k_words[0].rearrange("p n t -> p (n t)").bitcast(I32))
-        nc.sync.dma_start(q_late[:], q_rows[:, :, EARLY:NQ])
+        for n in range(2):
+            nc.sync.dma_start(q_late[n], q_rows[:, :, EARLY + n * P : EARLY + (n + 1) * P])
 
         warm = keep.tile([P, 1], F32, name="warm")
         nc.vector.memset(warm[:], 0.0)
@@ -74,16 +76,17 @@ def tile_attend_plq_sigts_topk_kernel(tc, qT, k_words, k_scales, ts, kb, offs, o
         q_codes = keep.tile([P, NQ], U32, name="q_codes", tag="scale_pool", align_bytes=64)
         q_sc = keep.tile([P, NQ], U8, name="q_sc", align_bytes=64)
 
-        def quantize_queries(raw, raw_lo, lo, hi):
-            q_bf = keep.tile([P, (hi - lo) * PACK], BF16, name="q_bf%d" % lo, tag="q_bf%d" % lo, align_bytes=64)
-            nc.scalar.copy(
-                q_bf[:].rearrange("p (c i t) -> p c t i", i=4, t=PACK),
-                raw[:, :, lo - raw_lo : hi - raw_lo].rearrange("p t (c i) -> p c t i", i=4),
-            )
+        def quantize_queries(parts, lo, hi):
+            q_bf = keep.tile([P, (hi - lo) * PACK], BF16, name="q_bf%d" % lo, align_bytes=64)
+            width = (hi - lo) * PACK // len(parts)
+            for n, raw in enumerate(parts):
+                nc.scalar.copy(
+                    q_bf[:, n * width : (n + 1) * width].rearrange("p (c i t) -> p c t i", i=4, t=PACK),
+                    raw.rearrange("p t (c i) -> p c t i", i=4),
+                )
             nc.vector.quantize_mx(out=q_codes[:, lo:hi].bitcast(FP8X4), scales=q_sc[:, lo:hi], in_=q_bf[:])
 
-        quantize_queries(q_early, 0, 0, HALF)
-        quantize_queries(q_early, 0, HALF, EARLY)
+        quantize_queries([q_early[:]], 0, EARLY)
 
         banks = []
         for n, rows in enumerate((ts_g, kb_g)):
@@ -112,20 +115,21 @@ def tile_attend_plq_sigts_topk_kernel(tc, qT, k_words, k_scales, ts, kb, offs, o
             words = keep.tile([P, HALF], U32, name="k_g%d" % h, align_bytes=64)
             nc.vector.tensor_copy(words[:], word_pool[:].indirect(offsets[:, 16 * h : 16 * (h + 1)]))
             k_g.append(words)
-        quantize_queries(q_late, EARLY, EARLY, NQ)
+        quantize_queries(q_late, EARLY, NQ)
 
         y_codes = keep.tile([P, SLOTS], U32, name="y_codes", align_bytes=64)
         y_sc = keep.tile([P, SLOTS], U8, name="y_sc", align_bytes=64)
         out_rows = out_0.rearrange("(p t) i -> p t i", t=PACK)
         out_words = out_1[0].rearrange("p i u -> p (i u)").bitcast(I32)
 
-        yT = [keep.tile([P, PACK, P], F32, name="yT%d" % s, align_bytes=64) for s in range(TILES)]
+        yT_pairs = [keep.tile([P, 2, PACK, P], F32, name="yT%d" % h, tag=("q_late", "yT1")[h], align_bytes=64) for h in range(2)]
+        yT = [yT_pairs[s // 2][:, s % 2] for s in range(TILES)]
         scores = [psum.tile([P, NQ], F32, name="score%d" % s, tag="score%d" % s) for s in range(TILES)]
 
-        late_scores = psum.tile([P, 2, LATE], F32, name="late_scores", tag="late")
+        late_scores = [psum.tile([P, LATE], F32, name="late_scores%d" % s, tag=("late", "turn2")[s]) for s in range(2)]
 
         def bank_of(s, lo, hi):
-            return late_scores[:, s, :] if lo == EARLY else scores[s][:, lo:hi]
+            return late_scores[s][:] if lo == EARLY and s < 2 else scores[s][:, lo:hi]
 
         def product(s, lo, hi):
             nc.tensor.matmul_mx(
@@ -147,16 +151,15 @@ def tile_attend_plq_sigts_topk_kernel(tc, qT, k_words, k_scales, ts, kb, offs, o
                 scale=col[:, 0, s : s + 1],
             )
 
+        for s in range(TILES):
+            product(s, 0, EARLY)
         for s in range(2):
-            product(s, 0, HALF)
-            product(s, HALF, EARLY)
             weigh(s, 0, EARLY)
-        for s in range(2):
+        for s in range(TILES):
             product(s, EARLY, NQ)
         for s in range(2):
             weigh(s, EARLY, NQ)
         for s in range(2, TILES):
-            product(s, 0, NQ)
             weigh(s, 0, NQ)
 
         y = [keep.tile([P, PACK, HALF], F32, name="y%d" % h) for h in range(2)]
@@ -208,8 +211,10 @@ def tile_attend_plq_sigts_topk_kernel(tc, qT, k_words, k_scales, ts, kb, offs, o
         turn(0, 2, 4, "turn2", False)
         store(0, 2, 4)
         turn_tile(2, 0, 4, "score0", True)
-        turn_tile(3, 0, 4, "score1", False)
-        store(1, 0, 4)
+        turn_tile(3, 0, 2, "score1", False)
+        store(1, 0, 2)
+        turn_tile(3, 2, 4, "late", False)
+        store(1, 2, 4)
         weave(0, 0, HALF, "v")
         weave(1, 0, 128, "v")
         weave(1, 128, HALF, "s")

@@ -73,7 +73,7 @@ def tile_attend_plq_sigts_topk_kernel(tc, qT, k_words, k_scales, ts, kb, offs, o
         nc.vector.tensor_copy(kb_g[:], kb_pool[:].indirect(offsets[:]))
         nc.vector.tensor_copy(k_sc[:], scale_pool[:].indirect(offsets[:]))
 
-        q_codes = keep.tile([P, NQ], U32, name="q_codes", tag="scale_pool", align_bytes=64)
+        q_codes = keep.tile([P, NQ], U32, name="q_codes", align_bytes=64)
         q_sc = keep.tile([P, NQ], U8, name="q_sc", align_bytes=64)
 
         def quantize_queries(parts, lo, hi):
@@ -97,18 +97,6 @@ def tile_attend_plq_sigts_topk_kernel(tc, qT, k_words, k_scales, ts, kb, offs, o
         col = keep.tile([P, 2, TILES], F32, name="col", tag="q_early")
         for n in range(2):
             nc.scalar.copy(col[:, n, :], banks[n][:, :, P - 1])
-
-        spare = psum.tile([P, 2, HALF], F32, name="spare", tag="turn2")
-        for n in range(2):
-            nc.tensor.matmul_mx(
-                out=spare[:, n, :],
-                lhsT=q_codes[:, 0:P].bitcast(FP8X4),
-                lhsT_scale=q_sc[:, 0:P],
-                rhs=q_codes[:, 0:HALF].bitcast(FP8X4),
-                rhs_scale=q_sc[:, 0:HALF],
-                start=True,
-                stop=True,
-            )
 
         k_g = []
         for h in range(2):

@@ -11,16 +11,13 @@ U16 = mybir.dt.uint16
 U8 = mybir.dt.uint8
 FP8X4 = mybir.dt.float8_e4m3fn_x4
 SIGMOID = mybir.ActivationFunctionType.Sigmoid
-MULT = mybir.AluOpType.mult
-ADD = mybir.AluOpType.add
+COPY = mybir.ActivationFunctionType.Copy
 
 P = 128
 PACK = 4
 D, NQ, SLOTS, TOKENS = 512, 512, 512, 2048
 TILES = SLOTS // P
 HALF = 256
-EARLY = 256
-LATE = NQ - EARLY
 FLOPS = 2 * D * NQ * SLOTS
 BYTES = 4 * D * NQ + 4 * P * TOKENS + 16 * TOKENS + 2 * 4 * TOKENS + 2 * P * 32 + 4 * NQ * SLOTS + NQ * SLOTS + 16 * SLOTS
 
@@ -34,17 +31,20 @@ def tile_attend_plq_sigts_topk_kernel(tc, qT, k_words, k_scales, ts, kb, offs, o
         offsets = keep.tile([P, SLOTS // 16], U16, name="offsets")
         ts_pool = keep.tile([P, TOKENS], F32, name="ts_pool")
         kb_pool = keep.tile([P, TOKENS], F32, name="kb_pool")
-        scale_pool = keep.tile([P, TOKENS], U8, name="scale_pool", tag="scale_pool", align_bytes=64)
+        scale_pool = keep.tile([P, TOKENS], U8, name="scale_pool", align_bytes=64)
         word_pool = keep.tile([P, TOKENS], U32, name="word_pool", align_bytes=64)
-        q_early = keep.tile([P, PACK, EARLY], F32, name="q_early", tag="q_early")
-        q_late_tile = keep.tile([P, 2, PACK, P], F32, name="q_late", tag="q_late", align_bytes=64)
-        q_late = [q_late_tile[:, n] for n in range(2)]
+        q_early = keep.tile([P, PACK, HALF], F32, name="q_early")
+        q_late = [keep.tile([P, PACK, P], F32, name="q_late%d" % n) for n in range(2)]
+
+        warm = keep.tile([P, 1], F32, name="warm")
+        nc.vector.memset(warm[:], 0.0)
+        nc.scalar.activation(warm[:], warm[:], SIGMOID)
 
         nc.gpsimd.memset(scale_pool[:].bitcast(I32), 0)
-        nc.vector.memset(ts_pool[0 : P - 1, 0:895], 0.0)
-        nc.vector.memset(ts_pool[0 : P - 1, 895:1792], 0.0)
-        nc.gpsimd.memset(ts_pool[0 : P - 1, 1792:TOKENS], 0.0)
-        nc.gpsimd.memset(kb_pool[0 : P - 1, :], 0.0)
+        for pool in (ts_pool, kb_pool):
+            nc.vector.memset(pool[0 : P - 1, 0:511], 0.0)
+            nc.vector.memset(pool[0 : P - 1, 511:1024], 0.0)
+            nc.gpsimd.memset(pool[0 : P - 1, 1024:TOKENS], 0.0)
         ident = keep.tile([P, P], F32, name="ident")
         make_identity(nc, ident[:])
 
@@ -52,7 +52,7 @@ def tile_attend_plq_sigts_topk_kernel(tc, qT, k_words, k_scales, ts, kb, offs, o
         nc.sync.dma_start(offsets[:], offs)
         nc.sync.dma_start(ts_pool[P - 1 : P, :], ts[0:1, :])
         nc.sync.dma_start(kb_pool[P - 1 : P, :], kb[0:1, :])
-        nc.sync.dma_start(q_early[:], q_rows[:, :, 0:EARLY])
+        nc.sync.dma_start(q_early[:], q_rows[:, :, 0:HALF])
         for quad in range(4):
             nc.sync.dma_start(
                 scale_pool[32 * quad : 32 * quad + 4, :].bitcast(I32),
@@ -60,152 +60,119 @@ def tile_attend_plq_sigts_topk_kernel(tc, qT, k_words, k_scales, ts, kb, offs, o
             )
         nc.sync.dma_start(word_pool[:].bitcast(I32), k_words[0].rearrange("p n t -> p (n t)").bitcast(I32))
         for n in range(2):
-            nc.sync.dma_start(q_late[n], q_rows[:, :, EARLY + n * P : EARLY + (n + 1) * P])
+            nc.sync.dma_start(q_late[n][:], q_rows[:, :, HALF + n * P : HALF + (n + 1) * P])
 
-        warm = keep.tile([P, 1], F32, name="warm")
-        nc.vector.memset(warm[:], 0.0)
-        nc.scalar.activation(warm[:], warm[:], SIGMOID)
-
-        ts_g = keep.tile([P, SLOTS], F32, name="ts_g")
-        kb_g = keep.tile([P, SLOTS], F32, name="kb_g")
-        k_sc = keep.tile([P, SLOTS], U8, name="k_sc", align_bytes=64)
-        nc.vector.tensor_copy(ts_g[:], ts_pool[:].indirect(offsets[:]))
-        nc.vector.tensor_copy(kb_g[:], kb_pool[:].indirect(offsets[:]))
-        nc.vector.tensor_copy(k_sc[:], scale_pool[:].indirect(offsets[:]))
+        col = keep.tile([P, 2, TILES], F32, name="col")
+        for n, pool in enumerate((ts_pool, kb_pool)):
+            rows = keep.tile([P, SLOTS], F32, name="rows%d" % n)
+            nc.scalar.activation(rows[:], pool[:].indirect(offsets[:]), COPY)
+            bank = psum.tile([P, TILES, P], F32, name="cols%d" % n, tag="late%d" % n)
+            for s in range(TILES):
+                nc.tensor.transpose(bank[:, s, :], rows[:, s * P : (s + 1) * P], ident[:])
+            nc.scalar.copy(col[:, n, :], bank[:, :, P - 1])
 
         q_codes = keep.tile([P, NQ], U32, name="q_codes", align_bytes=64)
         q_sc = keep.tile([P, NQ], U8, name="q_sc", align_bytes=64)
+
+        def interleave(engine, dst, src):
+            dst = dst.rearrange("p (c i t) -> p c t i", i=4, t=PACK)
+            src = src.rearrange("p t (c i) -> p c t i", i=4)
+            if engine == "v":
+                nc.vector.tensor_copy(dst, src)
+            else:
+                nc.scalar.copy(dst, src)
 
         def quantize_queries(parts, lo, hi):
             q_bf = keep.tile([P, (hi - lo) * PACK], BF16, name="q_bf%d" % lo, align_bytes=64)
             width = (hi - lo) * PACK // len(parts)
             for n, raw in enumerate(parts):
-                nc.scalar.copy(
-                    q_bf[:, n * width : (n + 1) * width].rearrange("p (c i t) -> p c t i", i=4, t=PACK),
-                    raw.rearrange("p t (c i) -> p c t i", i=4),
-                )
+                interleave("v", q_bf[:, n * width : (n + 1) * width], raw[:])
             nc.vector.quantize_mx(out=q_codes[:, lo:hi].bitcast(FP8X4), scales=q_sc[:, lo:hi], in_=q_bf[:])
 
-        quantize_queries([q_early[:]], 0, EARLY)
-
-        banks = []
-        for n, rows in enumerate((ts_g, kb_g)):
-            bank = psum.tile([P, TILES, P], F32, name="rows%d" % n, tag="turn%d" % n)
-            for s in range(TILES):
-                nc.tensor.transpose(bank[:, s, :], rows[:, s * P : (s + 1) * P], ident[:])
-            banks.append(bank)
-        col = keep.tile([P, 2, TILES], F32, name="col", tag="q_early")
-        for n in range(2):
-            nc.scalar.copy(col[:, n, :], banks[n][:, :, P - 1])
-
+        k_sc = keep.tile([P, SLOTS], U8, name="k_sc", align_bytes=64)
+        quantize_queries([q_early], 0, HALF)
+        nc.vector.tensor_copy(k_sc[:], scale_pool[:].indirect(offsets[:]))
         k_g = []
-        for h in range(2):
-            words = keep.tile([P, HALF], U32, name="k_g%d" % h, align_bytes=64)
-            nc.vector.tensor_copy(words[:], word_pool[:].indirect(offsets[:, 16 * h : 16 * (h + 1)]))
+        for s in range(TILES):
+            words = keep.tile([P, P], U32, name="k_g%d" % s, align_bytes=64)
+            nc.vector.tensor_copy(words[:], word_pool[:].indirect(offsets[:, 8 * s : 8 * (s + 1)]))
             k_g.append(words)
-        quantize_queries(q_late, EARLY, NQ)
+        quantize_queries(q_late, HALF, NQ)
 
         y_codes = keep.tile([P, SLOTS], U32, name="y_codes", align_bytes=64)
         y_sc = keep.tile([P, SLOTS], U8, name="y_sc", align_bytes=64)
         out_rows = out_0.rearrange("(p t) i -> p t i", t=PACK)
         out_words = out_1[0].rearrange("p i u -> p (i u)").bitcast(I32)
+        yT = [keep.tile([P, PACK, P], F32, name="yT%d" % s) for s in range(TILES)]
 
-        yT_pairs = [keep.tile([P, 2, PACK, P], F32, name="yT%d" % h, tag=("q_late", "yT1")[h], align_bytes=64) for h in range(2)]
-        yT = [yT_pairs[s // 2][:, s % 2] for s in range(TILES)]
-        scores = [psum.tile([P, NQ], F32, name="score%d" % s, tag="score%d" % s) for s in range(TILES)]
-
-        late_scores = [psum.tile([P, LATE], F32, name="late_scores%d" % s, tag=("late", "turn2")[s]) for s in range(2)]
-
-        def bank_of(s, lo, hi):
-            return late_scores[s][:] if lo == EARLY and s < 2 else scores[s][:, lo:hi]
-
-        def product(s, lo, hi):
-            nc.tensor.matmul_mx(
-                out=bank_of(s, lo, hi),
-                lhsT=k_g[s // 2][:, (s % 2) * P : (s % 2 + 1) * P].bitcast(FP8X4),
-                lhsT_scale=k_sc[:, s * P : (s + 1) * P],
-                rhs=q_codes[:, lo:hi].bitcast(FP8X4),
-                rhs_scale=q_sc[:, lo:hi],
-                start=True,
-                stop=True,
-            )
-
-        def weigh(s, lo, hi):
-            nc.scalar.activation(
-                yT[s][:, :, lo // PACK : hi // PACK],
-                bank_of(s, lo, hi).rearrange("p (m t) -> p t m", t=PACK),
-                SIGMOID,
-                bias=col[:, 1, s : s + 1],
-                scale=col[:, 0, s : s + 1],
-            )
-
-        for s in range(TILES):
-            product(s, 0, EARLY)
-        for s in range(2):
-            weigh(s, 0, EARLY)
-        for s in range(TILES):
-            product(s, EARLY, NQ)
-        for s in range(2):
-            weigh(s, EARLY, NQ)
-        for s in range(2, TILES):
-            weigh(s, 0, NQ)
+        for part, lo in (("early", 0), ("late", HALF)):
+            banks = [psum.tile([P, HALF], F32, name="%s_scores%d" % (part, s), tag="%s%d" % (part, s)) for s in range(TILES)]
+            for s in range(TILES):
+                nc.tensor.matmul_mx(
+                    out=banks[s][:],
+                    lhsT=k_g[s][:].bitcast(FP8X4),
+                    lhsT_scale=k_sc[:, s * P : (s + 1) * P],
+                    rhs=q_codes[:, lo : lo + HALF].bitcast(FP8X4),
+                    rhs_scale=q_sc[:, lo : lo + HALF],
+                    start=True,
+                    stop=True,
+                )
+            for s in range(TILES):
+                nc.scalar.activation(
+                    yT[s][:, :, lo // PACK : (lo + HALF) // PACK],
+                    banks[s][:].rearrange("p (m t) -> p t m", t=PACK),
+                    SIGMOID,
+                    bias=col[:, 1, s : s + 1],
+                    scale=col[:, 0, s : s + 1],
+                )
 
         y = [keep.tile([P, PACK, HALF], F32, name="y%d" % h) for h in range(2)]
         y_bf = [keep.tile([P, HALF * PACK], BF16, name="y_bf%d" % h, align_bytes=64) for h in range(2)]
+
+        def empty(dst, src, on_vector):
+            if on_vector:
+                nc.vector.tensor_copy(dst, src)
+            else:
+                nc.scalar.copy(dst, src)
 
         def turn(h, lo, hi, tag, on_vector):
             bank = psum.tile([P, hi - lo, 2, P], F32, name="turned%d_%d" % (h, lo), tag=tag)
             for t in range(lo, hi):
                 for s in range(2):
                     nc.tensor.transpose(bank[:, t - lo, s, :], yT[2 * h + s][:, t, :], ident[:])
-            src = bank[:].rearrange("p u s i -> p u (s i)")
-            if on_vector:
-                nc.vector.tensor_copy(y[h][:, lo:hi, :], src)
-            else:
-                nc.scalar.copy(y[h][:, lo:hi, :], src)
+            empty(y[h][:, lo:hi, :], bank[:].rearrange("p u s i -> p u (s i)"), on_vector)
+
+        def turn_tile(s, lo, hi, tag, on_vector):
+            bank = psum.tile([P, hi - lo, P], F32, name="turned_tile%d_%d" % (s, lo), tag=tag)
+            for t in range(lo, hi):
+                nc.tensor.transpose(bank[:, t - lo, :], yT[s][:, t, :], ident[:])
+            empty(y[1][:, lo:hi, (s % 2) * P : (s % 2 + 1) * P], bank[:], on_vector)
 
         def store(h, lo, hi):
             nc.sync.dma_start(out_rows[:, lo:hi, h * HALF : (h + 1) * HALF], y[h][:, lo:hi, :])
 
         def weave(h, lo, hi, engine):
-            dst = y_bf[h][:, lo * PACK : hi * PACK].rearrange("p (c i t) -> p c t i", i=4, t=PACK)
-            src = y[h][:, :, lo:hi].rearrange("p t (c i) -> p c t i", i=4)
-            if engine == "v":
-                nc.vector.tensor_copy(dst, src)
-            elif engine == "g":
-                nc.gpsimd.tensor_copy(dst, src)
-            else:
-                nc.scalar.copy(dst, src)
+            interleave(engine, y_bf[h][:, lo * PACK : hi * PACK], y[h][:, :, lo:hi])
 
         def quantize(h):
             half = slice(h * HALF, (h + 1) * HALF)
             nc.vector.quantize_mx(out=y_codes[:, half].bitcast(FP8X4), scales=y_sc[:, half], in_=y_bf[h][:])
             nc.sync.dma_start(out_words[:, half], y_codes[:, half].bitcast(I32))
 
-        def turn_tile(s, lo, hi, tag, on_vector):
-            bank = psum.tile([P, hi - lo, P], F32, name="turned_tile%d_%d" % (s, lo), tag=tag)
-            for t in range(lo, hi):
-                nc.tensor.transpose(bank[:, t - lo, :], yT[s][:, t, :], ident[:])
-            dst = y[1][:, lo:hi, (s % 2) * P : (s % 2 + 1) * P]
-            if on_vector:
-                nc.vector.tensor_copy(dst, bank[:])
-            else:
-                nc.scalar.copy(dst, bank[:])
-
-        turn(0, 0, 1, "turn0", True)
+        turn(0, 0, 1, "early0", True)
         store(0, 0, 1)
-        turn(0, 1, 2, "turn1", True)
+        turn(0, 1, 2, "early1", True)
         store(0, 1, 2)
-        turn(0, 2, 4, "turn2", False)
+        turn(0, 2, 4, "early2", False)
         store(0, 2, 4)
-        turn_tile(2, 0, 4, "score0", True)
-        turn_tile(3, 0, 2, "score1", False)
+        turn_tile(2, 0, 4, "early3", True)
+        turn_tile(3, 0, 2, "late0", False)
         store(1, 0, 2)
-        turn_tile(3, 2, 4, "late", False)
+        turn_tile(3, 2, 4, "late1", False)
         store(1, 2, 4)
         weave(0, 0, HALF, "v")
-        weave(1, 0, 128, "v")
-        weave(1, 128, HALF, "s")
+        weave(1, 0, P, "v")
+        weave(1, P, HALF, "s")
         quantize(0)
         quantize(1)
         for quad in range(4):

@@ -34,7 +34,7 @@ def tile_attend_plq_sigts_topk_kernel(tc, qT, k_words, k_scales, ts, kb, offs, o
         scale_pool = keep.tile([P, TOKENS], U8, name="scale_pool", align_bytes=64)
         word_pool = keep.tile([P, TOKENS], U32, name="word_pool", align_bytes=64)
         q_early = keep.tile([P, PACK, HALF], F32, name="q_early")
-        q_late = [keep.tile([P, PACK, P], F32, name="q_late%d" % n) for n in range(2)]
+        q_late = [keep.tile([P, PACK, P], F32, name="q_late%d" % n, tag="q_late%d" % n) for n in range(2)]
 
         warm = keep.tile([P, 1], F32, name="warm")
         nc.vector.memset(warm[:], 0.0)
@@ -82,28 +82,29 @@ def tile_attend_plq_sigts_topk_kernel(tc, qT, k_words, k_scales, ts, kb, offs, o
             else:
                 nc.scalar.copy(dst, src)
 
-        def quantize_queries(parts, lo, hi):
+        def quantize_queries(parts, engines, lo, hi):
             q_bf = keep.tile([P, (hi - lo) * PACK], BF16, name="q_bf%d" % lo, align_bytes=64)
             width = (hi - lo) * PACK // len(parts)
             for n, raw in enumerate(parts):
-                interleave("v", q_bf[:, n * width : (n + 1) * width], raw[:])
+                interleave(engines[n], q_bf[:, n * width : (n + 1) * width], raw[:])
             nc.vector.quantize_mx(out=q_codes[:, lo:hi].bitcast(FP8X4), scales=q_sc[:, lo:hi], in_=q_bf[:])
 
         k_sc = keep.tile([P, SLOTS], U8, name="k_sc", align_bytes=64)
-        quantize_queries([q_early], 0, HALF)
+        quantize_queries([q_early], "v", 0, HALF)
         nc.vector.tensor_copy(k_sc[:], scale_pool[:].indirect(offsets[:]))
         k_g = []
         for s in range(TILES):
             words = keep.tile([P, P], U32, name="k_g%d" % s, align_bytes=64)
             nc.vector.tensor_copy(words[:], word_pool[:].indirect(offsets[:, 8 * s : 8 * (s + 1)]))
             k_g.append(words)
-        quantize_queries(q_late, HALF, NQ)
+        quantize_queries(q_late, "sv", HALF, NQ)
 
         y_codes = keep.tile([P, SLOTS], U32, name="y_codes", align_bytes=64)
         y_sc = keep.tile([P, SLOTS], U8, name="y_sc", align_bytes=64)
         out_rows = out_0.rearrange("(p t) i -> p t i", t=PACK)
         out_words = out_1[0].rearrange("p i u -> p (i u)").bitcast(I32)
-        yT = [keep.tile([P, PACK, P], F32, name="yT%d" % s) for s in range(TILES)]
+        yT_all = keep.tile([P, TILES, PACK, P], F32, name="yT", tag="q_late0")
+        yT = [yT_all[:, s] for s in range(TILES)]
 
         for part, lo in (("early", 0), ("late", HALF)):
             banks = [psum.tile([P, HALF], F32, name="%s_scores%d" % (part, s), tag="%s%d" % (part, s)) for s in range(TILES)]
@@ -159,21 +160,18 @@ def tile_attend_plq_sigts_topk_kernel(tc, qT, k_words, k_scales, ts, kb, offs, o
             nc.vector.quantize_mx(out=y_codes[:, half].bitcast(FP8X4), scales=y_sc[:, half], in_=y_bf[h][:])
             nc.sync.dma_start(out_words[:, half], y_codes[:, half].bitcast(I32))
 
-        turn(0, 0, 1, "early0", True)
-        store(0, 0, 1)
-        turn(0, 1, 2, "early1", True)
-        store(0, 1, 2)
-        turn(0, 2, 4, "early2", False)
-        store(0, 2, 4)
-        turn_tile(2, 0, 4, "early3", True)
-        turn_tile(3, 0, 2, "late0", False)
+        for t in range(PACK):
+            turn(0, t, t + 1, "early%d" % t, t % 2 == 0)
+            store(0, t, t + 1)
+        turn_tile(2, 0, 4, "late0", False)
+        turn_tile(3, 0, 2, "late1", False)
         store(1, 0, 2)
-        turn_tile(3, 2, 4, "late1", False)
+        turn_tile(3, 2, 4, "late2", False)
         store(1, 2, 4)
         weave(0, 0, HALF, "v")
         weave(1, 0, P, "v")
-        weave(1, P, HALF, "s")
         quantize(0)
+        weave(1, P, HALF, "v")
         quantize(1)
         for quad in range(4):
             queue = nc.scalar if quad % 2 == 0 else nc.sync

@@ -36,6 +36,12 @@ def tile_attend_plq_sigts_topk_kernel(tc, qT, k_words, k_scales, ts, kb, offs, o
         q_early = keep.tile([P, PACK, HALF], F32, name="q_early")
         q_late = [keep.tile([P, PACK, P], F32, name="q_late%d" % n, tag="q_late%d" % n) for n in range(2)]
 
+        q_rows = qT[0].rearrange("(p j) c -> p j c", j=PACK)
+        nc.sync.dma_start(offsets[:], offs)
+        nc.scalar.dma_start(ts_pool[P - 1 : P, :], ts[0:1, :])
+        nc.sync.dma_start(kb_pool[P - 1 : P, :], kb[0:1, :])
+        nc.scalar.dma_start(q_early[:], q_rows[:, :, 0:HALF])
+
         warm = keep.tile([P, 1], F32, name="warm")
         nc.vector.memset(warm[:], 0.0)
         nc.scalar.activation(warm[:], warm[:], SIGMOID)
@@ -48,11 +54,6 @@ def tile_attend_plq_sigts_topk_kernel(tc, qT, k_words, k_scales, ts, kb, offs, o
         ident = keep.tile([P, P], F32, name="ident")
         make_identity(nc, ident[:])
 
-        q_rows = qT[0].rearrange("(p j) c -> p j c", j=PACK)
-        nc.sync.dma_start(offsets[:], offs)
-        nc.sync.dma_start(ts_pool[P - 1 : P, :], ts[0:1, :])
-        nc.sync.dma_start(kb_pool[P - 1 : P, :], kb[0:1, :])
-        nc.sync.dma_start(q_early[:], q_rows[:, :, 0:HALF])
         for quad in range(4):
             nc.sync.dma_start(
                 scale_pool[32 * quad : 32 * quad + 4, :].bitcast(I32),
@@ -62,14 +63,18 @@ def tile_attend_plq_sigts_topk_kernel(tc, qT, k_words, k_scales, ts, kb, offs, o
         for n in range(2):
             nc.sync.dma_start(q_late[n][:], q_rows[:, :, HALF + n * P : HALF + (n + 1) * P])
 
-        col = keep.tile([P, 2, TILES], F32, name="col")
+        rows = []
         for n, pool in enumerate((ts_pool, kb_pool)):
-            rows = keep.tile([P, SLOTS], F32, name="rows%d" % n)
-            nc.scalar.activation(rows[:], pool[:].indirect(offsets[:]), COPY)
-            bank = psum.tile([P, TILES, P], F32, name="cols%d" % n, tag="late%d" % n)
+            row = keep.tile([P, SLOTS], F32, name="rows%d" % n, tag="rows%d" % n, align_bytes=64)
+            nc.scalar.activation(row[:], pool[:].indirect(offsets[:]), COPY)
+            rows.append(row)
+        col = keep.tile([P, TILES, 2], F32, name="col")
+        col_banks = [psum.tile([P, 2, P], F32, name="cols%d" % s, tag="early%d" % s) for s in range(TILES)]
+        for n in range(2):
             for s in range(TILES):
-                nc.tensor.transpose(bank[:, s, :], rows[:, s * P : (s + 1) * P], ident[:])
-            nc.scalar.copy(col[:, n, :], bank[:, :, P - 1])
+                nc.tensor.transpose(col_banks[s][:, n, :], rows[n][:, s * P : (s + 1) * P], ident[:])
+        for s in range(TILES):
+            nc.scalar.copy(col[:, s, :], col_banks[s][:, :, P - 1])
 
         q_codes = keep.tile([P, NQ], U32, name="q_codes", align_bytes=64)
         q_sc = keep.tile([P, NQ], U8, name="q_sc", align_bytes=64)
@@ -83,7 +88,7 @@ def tile_attend_plq_sigts_topk_kernel(tc, qT, k_words, k_scales, ts, kb, offs, o
                 nc.scalar.copy(dst, src)
 
         def quantize_queries(parts, engines, lo, hi):
-            q_bf = keep.tile([P, (hi - lo) * PACK], BF16, name="q_bf%d" % lo, align_bytes=64)
+            q_bf = keep.tile([P, (hi - lo) * PACK], BF16, name="q_bf%d" % lo, tag="q_bf0" if lo == 0 else "rows1", align_bytes=64)
             width = (hi - lo) * PACK // len(parts)
             for n, raw in enumerate(parts):
                 interleave(engines[n], q_bf[:, n * width : (n + 1) * width], raw[:])
@@ -123,8 +128,8 @@ def tile_attend_plq_sigts_topk_kernel(tc, qT, k_words, k_scales, ts, kb, offs, o
                     yT[s][:, :, lo // PACK : (lo + HALF) // PACK],
                     banks[s][:].rearrange("p (m t) -> p t m", t=PACK),
                     SIGMOID,
-                    bias=col[:, 1, s : s + 1],
-                    scale=col[:, 0, s : s + 1],
+                    bias=col[:, s, 1:2],
+                    scale=col[:, s, 0:1],
                 )
 
         y = [keep.tile([P, PACK, HALF], F32, name="y%d" % h) for h in range(2)]

@@ -37,10 +37,10 @@ def tile_attend_plq_sigts_topk_kernel(tc, qT, k_words, k_scales, ts, kb, offs, o
         q_late = [keep.tile([P, PACK, P], F32, name="q_late%d" % n, tag="q_late%d" % n) for n in range(2)]
 
         q_rows = qT[0].rearrange("(p j) c -> p j c", j=PACK)
-        nc.sync.dma_start(offsets[:], offs)
-        nc.scalar.dma_start(ts_pool[P - 1 : P, :], ts[0:1, :])
+        nc.sync.dma_start(ts_pool[P - 1 : P, :], ts[0:1, :])
         nc.sync.dma_start(kb_pool[P - 1 : P, :], kb[0:1, :])
-        nc.scalar.dma_start(q_early[:], q_rows[:, :, 0:HALF])
+        nc.sync.dma_start(offsets[:], offs)
+        nc.sync.dma_start(q_early[:], q_rows[:, :, 0:HALF])
 
         warm = keep.tile([P, 1], F32, name="warm")
         nc.vector.memset(warm[:], 0.0)
@@ -54,11 +54,8 @@ def tile_attend_plq_sigts_topk_kernel(tc, qT, k_words, k_scales, ts, kb, offs, o
         ident = keep.tile([P, P], F32, name="ident")
         make_identity(nc, ident[:])
 
-        for quad in range(4):
-            nc.sync.dma_start(
-                scale_pool[32 * quad : 32 * quad + 4, :].bitcast(I32),
-                k_scales[0][4 * quad : 4 * quad + 4, :].bitcast(I32),
-            )
+        for r in range(4):
+            nc.sync.dma_start(scale_pool[r:P:32, :].bitcast(I32), k_scales[0][r:16:4, :].bitcast(I32))
         nc.sync.dma_start(word_pool[:].bitcast(I32), k_words[0].rearrange("p n t -> p (n t)").bitcast(I32))
         for n in range(2):
             nc.sync.dma_start(q_late[n][:], q_rows[:, :, HALF + n * P : HALF + (n + 1) * P])
@@ -160,24 +157,32 @@ def tile_attend_plq_sigts_topk_kernel(tc, qT, k_words, k_scales, ts, kb, offs, o
         def weave(h, lo, hi, engine):
             interleave(engine, y_bf[h][:, lo * PACK : hi * PACK], y[h][:, :, lo:hi])
 
-        def quantize(h):
-            half = slice(h * HALF, (h + 1) * HALF)
-            nc.vector.quantize_mx(out=y_codes[:, half].bitcast(FP8X4), scales=y_sc[:, half], in_=y_bf[h][:])
-            nc.sync.dma_start(out_words[:, half], y_codes[:, half].bitcast(I32))
+        def quantize(lo, hi):
+            h = lo // HALF
+            src = y_bf[h][:, (lo - h * HALF) * PACK : (hi - h * HALF) * PACK]
+            nc.vector.quantize_mx(out=y_codes[:, lo:hi].bitcast(FP8X4), scales=y_sc[:, lo:hi], in_=src)
+
+        def store_words(lo, hi):
+            nc.sync.dma_start(out_words[:, lo:hi], y_codes[:, lo:hi].bitcast(I32))
 
         for t in range(PACK):
             turn(0, t, t + 1, "early%d" % t, t % 2 == 0)
             store(0, t, t + 1)
-        turn_tile(2, 0, 4, "late0", False)
-        turn_tile(3, 0, 2, "late1", False)
+        turn_tile(2, 0, 2, "late0", False)
+        turn_tile(2, 2, 4, "late1", False)
+        turn_tile(3, 0, 2, "late2", False)
         store(1, 0, 2)
-        turn_tile(3, 2, 4, "late2", False)
+        turn_tile(3, 2, 4, "late3", False)
         store(1, 2, 4)
         weave(0, 0, HALF, "v")
         weave(1, 0, P, "v")
-        quantize(0)
-        weave(1, P, HALF, "v")
-        quantize(1)
+        quantize(0, HALF)
+        quantize(HALF, 3 * P)
+        store_words(0, 3 * P)
+        weave(1, P, P + 32, "v")
+        weave(1, P + 32, HALF, "s")
+        quantize(3 * P, SLOTS)
+        store_words(3 * P, SLOTS)
         for quad in range(4):
             queue = nc.scalar if quad % 2 == 0 else nc.sync
             queue.dma_start(

@@ -60,18 +60,16 @@ def tile_attend_plq_sigts_topk_kernel(tc, qT, k_words, k_scales, ts, kb, offs, o
         for n in range(2):
             nc.sync.dma_start(q_late[n][:], q_rows[:, :, HALF + n * P : HALF + (n + 1) * P])
 
-        rows = []
+        after_late = keep.tile([P, TILES * NQ + 2 * TILES], F32, name="after_late", tag="q_late1")
+        col = after_late[:, TILES * NQ :].rearrange("p (n s) -> p n s", n=2)
+        yT = [after_late[:, s * NQ : (s + 1) * NQ].rearrange("p (t m) -> p t m", t=PACK) for s in range(TILES)]
         for n, pool in enumerate((ts_pool, kb_pool)):
-            row = keep.tile([P, SLOTS], F32, name="rows%d" % n, tag="rows%d" % n, align_bytes=64)
+            row = keep.tile([P, SLOTS], F32, name="rows%d" % n)
             nc.scalar.activation(row[:], pool[:].indirect(offsets[:]), COPY)
-            rows.append(row)
-        col = keep.tile([P, TILES, 2], F32, name="col")
-        col_banks = [psum.tile([P, 2, P], F32, name="cols%d" % s, tag="early%d" % s) for s in range(TILES)]
-        for n in range(2):
+            bank = psum.tile([P, TILES, P], F32, name="cols%d" % n, tag="turn%d" % n)
             for s in range(TILES):
-                nc.tensor.transpose(col_banks[s][:, n, :], rows[n][:, s * P : (s + 1) * P], ident[:])
-        for s in range(TILES):
-            nc.scalar.copy(col[:, s, :], col_banks[s][:, :, P - 1])
+                nc.tensor.transpose(bank[:, s, :], row[:, s * P : (s + 1) * P], ident[:])
+            nc.scalar.copy(col[:, n, :], bank[:, :, P - 1])
 
         q_codes = keep.tile([P, NQ], U32, name="q_codes", align_bytes=64)
         q_sc = keep.tile([P, NQ], U8, name="q_sc", align_bytes=64)
@@ -84,50 +82,61 @@ def tile_attend_plq_sigts_topk_kernel(tc, qT, k_words, k_scales, ts, kb, offs, o
             else:
                 nc.scalar.copy(dst, src)
 
-        def quantize_queries(parts, engines, lo, hi):
-            q_bf = keep.tile([P, (hi - lo) * PACK], BF16, name="q_bf%d" % lo, tag="q_bf0" if lo == 0 else "rows1", align_bytes=64)
-            width = (hi - lo) * PACK // len(parts)
-            for n, raw in enumerate(parts):
-                interleave(engines[n], q_bf[:, n * width : (n + 1) * width], raw[:])
+        def quantize_queries(raw, engine, lo, hi):
+            q_bf = keep.tile([P, (hi - lo) * PACK], BF16, name="q_bf%d" % lo, align_bytes=64)
+            interleave(engine, q_bf[:], raw[:])
             nc.vector.quantize_mx(out=q_codes[:, lo:hi].bitcast(FP8X4), scales=q_sc[:, lo:hi], in_=q_bf[:])
 
         k_sc = keep.tile([P, SLOTS], U8, name="k_sc", align_bytes=64)
-        quantize_queries([q_early], "v", 0, HALF)
+        quantize_queries(q_early, "v", 0, HALF)
         nc.vector.tensor_copy(k_sc[:], scale_pool[:].indirect(offsets[:]))
         k_g = []
-        for s in range(TILES):
-            words = keep.tile([P, P], U32, name="k_g%d" % s, align_bytes=64)
-            nc.vector.tensor_copy(words[:], word_pool[:].indirect(offsets[:, 8 * s : 8 * (s + 1)]))
+        for h in range(2):
+            words = keep.tile([P, HALF], U32, name="k_g%d" % h, align_bytes=64)
+            nc.vector.tensor_copy(words[:], word_pool[:].indirect(offsets[:, 16 * h : 16 * (h + 1)]))
             k_g.append(words)
-        quantize_queries(q_late, "sv", HALF, NQ)
+        for n in range(2):
+            quantize_queries(q_late[n], "s", HALF + n * P, HALF + (n + 1) * P)
 
         y_codes = keep.tile([P, SLOTS], U32, name="y_codes", align_bytes=64)
         y_sc = keep.tile([P, SLOTS], U8, name="y_sc", align_bytes=64)
         out_rows = out_0.rearrange("(p t) i -> p t i", t=PACK)
         out_words = out_1[0].rearrange("p i u -> p (i u)").bitcast(I32)
-        yT_all = keep.tile([P, TILES, PACK, P], F32, name="yT", tag="q_late0")
-        yT = [yT_all[:, s] for s in range(TILES)]
+        early = [psum.tile([P, HALF], F32, name="early%d" % s, tag="early%d" % s) for s in range(2)]
+        late = [psum.tile([P, HALF], F32, name="late%d" % s, tag="late%d" % s) for s in range(2)]
+        whole = [psum.tile([P, NQ], F32, name="whole%d" % s, tag="whole%d" % s) for s in range(2)]
 
-        for part, lo in (("early", 0), ("late", HALF)):
-            banks = [psum.tile([P, HALF], F32, name="%s_scores%d" % (part, s), tag="%s%d" % (part, s)) for s in range(TILES)]
+        def bank_of(s, lo, hi):
+            if s >= 2:
+                return whole[s - 2][:, lo:hi]
+            return early[s][:, lo:hi] if lo < HALF else late[s][:, lo - HALF : hi - HALF]
+
+        def weigh(s, lo, hi):
+            nc.scalar.activation(
+                yT[s][:, :, lo // PACK : hi // PACK],
+                bank_of(s, lo, hi).rearrange("p (m t) -> p t m", t=PACK),
+                SIGMOID,
+                bias=col[:, 1, s : s + 1],
+                scale=col[:, 0, s : s + 1],
+            )
+
+        for lo, hi in ((0, HALF), (HALF, HALF + P), (HALF + P, NQ)):
             for s in range(TILES):
                 nc.tensor.matmul_mx(
-                    out=banks[s][:],
-                    lhsT=k_g[s][:].bitcast(FP8X4),
+                    out=bank_of(s, lo, hi),
+                    lhsT=k_g[s // 2][:, (s % 2) * P : (s % 2 + 1) * P].bitcast(FP8X4),
                     lhsT_scale=k_sc[:, s * P : (s + 1) * P],
-                    rhs=q_codes[:, lo : lo + HALF].bitcast(FP8X4),
-                    rhs_scale=q_sc[:, lo : lo + HALF],
+                    rhs=q_codes[:, lo:hi].bitcast(FP8X4),
+                    rhs_scale=q_sc[:, lo:hi],
                     start=True,
                     stop=True,
                 )
-            for s in range(TILES):
-                nc.scalar.activation(
-                    yT[s][:, :, lo // PACK : (lo + HALF) // PACK],
-                    banks[s][:].rearrange("p (m t) -> p t m", t=PACK),
-                    SIGMOID,
-                    bias=col[:, s, 1:2],
-                    scale=col[:, s, 0:1],
-                )
+        for s in range(2):
+            weigh(s, 0, HALF)
+        for s in range(2):
+            weigh(s, HALF, NQ)
+        for s in range(2, TILES):
+            weigh(s, 0, NQ)
 
         y = [keep.tile([P, PACK, HALF], F32, name="y%d" % h) for h in range(2)]
         y_bf = [keep.tile([P, HALF * PACK], BF16, name="y_bf%d" % h, align_bytes=64) for h in range(2)]
@@ -149,10 +158,13 @@ def tile_attend_plq_sigts_topk_kernel(tc, qT, k_words, k_scales, ts, kb, offs, o
             bank = psum.tile([P, hi - lo, P], F32, name="turned_tile%d_%d" % (s, lo), tag=tag)
             for t in range(lo, hi):
                 nc.tensor.transpose(bank[:, t - lo, :], yT[s][:, t, :], ident[:])
-            empty(y[1][:, lo:hi, (s % 2) * P : (s % 2 + 1) * P], bank[:], on_vector)
+            empty(y[s // 2][:, lo:hi, (s % 2) * P : (s % 2 + 1) * P], bank[:], on_vector)
 
         def store(h, lo, hi):
             nc.sync.dma_start(out_rows[:, lo:hi, h * HALF : (h + 1) * HALF], y[h][:, lo:hi, :])
+
+        def store_tile(s, lo, hi):
+            nc.sync.dma_start(out_rows[:, lo:hi, s * P : (s + 1) * P], y[s // 2][:, lo:hi, (s % 2) * P : (s % 2 + 1) * P])
 
         def weave(h, lo, hi, engine):
             interleave(engine, y_bf[h][:, lo * PACK : hi * PACK], y[h][:, :, lo:hi])
@@ -165,14 +177,18 @@ def tile_attend_plq_sigts_topk_kernel(tc, qT, k_words, k_scales, ts, kb, offs, o
         def store_words(lo, hi):
             nc.sync.dma_start(out_words[:, lo:hi], y_codes[:, lo:hi].bitcast(I32))
 
-        for t in range(PACK):
-            turn(0, t, t + 1, "early%d" % t, t % 2 == 0)
-            store(0, t, t + 1)
+        turn_tile(0, 0, 2, "turn0", True)
+        store_tile(0, 0, 2)
+        turn_tile(1, 0, 2, "turn1", True)
+        store_tile(1, 0, 2)
+        turn(0, 2, 3, "early0", True)
+        turn(0, 3, 4, "early1", False)
+        store(0, 2, 4)
         turn_tile(2, 0, 2, "late0", False)
         turn_tile(2, 2, 4, "late1", False)
-        turn_tile(3, 0, 2, "late2", False)
+        turn_tile(3, 0, 2, "whole0", False)
         store(1, 0, 2)
-        turn_tile(3, 2, 4, "late3", False)
+        turn_tile(3, 2, 4, "whole1", False)
         store(1, 2, 4)
         weave(0, 0, HALF, "v")
         weave(1, 0, P, "v")

@@ -12,6 +12,8 @@ U8 = mybir.dt.uint8
 FP8X4 = mybir.dt.float8_e4m3fn_x4
 SIGMOID = mybir.ActivationFunctionType.Sigmoid
 COPY = mybir.ActivationFunctionType.Copy
+MULT = mybir.AluOpType.mult
+ADD = mybir.AluOpType.add
 
 P = 128
 PACK = 4
@@ -66,7 +68,7 @@ def tile_attend_plq_sigts_topk_kernel(tc, qT, k_words, k_scales, ts, kb, offs, o
         for n, pool in enumerate((ts_pool, kb_pool)):
             row = keep.tile([P, SLOTS], F32, name="rows%d" % n)
             nc.scalar.activation(row[:], pool[:].indirect(offsets[:]), COPY)
-            bank = psum.tile([P, TILES, P], F32, name="cols%d" % n, tag="turn%d" % n)
+            bank = psum.tile([P, TILES, P], F32, name="cols%d" % n, tag="late%d" % (2 + n))
             for s in range(TILES):
                 nc.tensor.transpose(bank[:, s, :], row[:, s * P : (s + 1) * P], ident[:])
             nc.scalar.copy(col[:, n, :], bank[:, :, P - 1])
@@ -102,41 +104,41 @@ def tile_attend_plq_sigts_topk_kernel(tc, qT, k_words, k_scales, ts, kb, offs, o
         y_sc = keep.tile([P, SLOTS], U8, name="y_sc", align_bytes=64)
         out_rows = out_0.rearrange("(p t) i -> p t i", t=PACK)
         out_words = out_1[0].rearrange("p i u -> p (i u)").bitcast(I32)
-        early = [psum.tile([P, HALF], F32, name="early%d" % s, tag="early%d" % s) for s in range(2)]
-        late = [psum.tile([P, HALF], F32, name="late%d" % s, tag="late%d" % s) for s in range(2)]
-        whole = [psum.tile([P, NQ], F32, name="whole%d" % s, tag="whole%d" % s) for s in range(2)]
+        early = [psum.tile([P, HALF], F32, name="early%d" % s, tag="early%d" % s) for s in range(TILES)]
+        late = [psum.tile([P, HALF], F32, name="late%d" % s, tag="late%d" % s) for s in range(TILES)]
 
         def bank_of(s, lo, hi):
-            if s >= 2:
-                return whole[s - 2][:, lo:hi]
             return early[s][:, lo:hi] if lo < HALF else late[s][:, lo - HALF : hi - HALF]
 
-        def weigh(s, lo, hi):
-            nc.scalar.activation(
-                yT[s][:, :, lo // PACK : hi // PACK],
-                bank_of(s, lo, hi).rearrange("p (m t) -> p t m", t=PACK),
-                SIGMOID,
-                bias=col[:, 1, s : s + 1],
-                scale=col[:, 0, s : s + 1],
+        def product(s, lo, hi):
+            nc.tensor.matmul_mx(
+                out=bank_of(s, lo, hi),
+                lhsT=k_g[s // 2][:, (s % 2) * P : (s % 2 + 1) * P].bitcast(FP8X4),
+                lhsT_scale=k_sc[:, s * P : (s + 1) * P],
+                rhs=q_codes[:, lo:hi].bitcast(FP8X4),
+                rhs_scale=q_sc[:, lo:hi],
+                start=True,
+                stop=True,
             )
 
-        for lo, hi in ((0, HALF), (HALF, HALF + P), (HALF + P, NQ)):
-            for s in range(TILES):
-                nc.tensor.matmul_mx(
-                    out=bank_of(s, lo, hi),
-                    lhsT=k_g[s // 2][:, (s % 2) * P : (s % 2 + 1) * P].bitcast(FP8X4),
-                    lhsT_scale=k_sc[:, s * P : (s + 1) * P],
-                    rhs=q_codes[:, lo:hi].bitcast(FP8X4),
-                    rhs_scale=q_sc[:, lo:hi],
-                    start=True,
-                    stop=True,
-                )
-        for s in range(2):
-            weigh(s, 0, HALF)
-        for s in range(2):
-            weigh(s, HALF, NQ)
+        def weigh(s, lo, hi):
+            dst = yT[s][:, :, lo // PACK : hi // PACK]
+            src = bank_of(s, lo, hi).rearrange("p (m t) -> p t m", t=PACK)
+            if s < 2:
+                nc.scalar.activation(dst, src, SIGMOID, bias=col[:, 1, s : s + 1], scale=col[:, 0, s : s + 1])
+            else:
+                nc.vector.tensor_scalar(dst, src, col[:, 0, s : s + 1], col[:, 1, s : s + 1], MULT, ADD)
+
+        for s in range(TILES):
+            product(s, 0, HALF)
+        for lo in (HALF, HALF + P):
+            for s in range(2):
+                product(s, lo, lo + P)
         for s in range(2, TILES):
-            weigh(s, 0, NQ)
+            product(s, HALF, NQ)
+        for lo in (0, HALF):
+            for s in range(TILES):
+                weigh(s, lo, lo + HALF)
 
         y = [keep.tile([P, PACK, HALF], F32, name="y%d" % h) for h in range(2)]
         y_bf = [keep.tile([P, HALF * PACK], BF16, name="y_bf%d" % h, align_bytes=64) for h in range(2)]
@@ -158,7 +160,11 @@ def tile_attend_plq_sigts_topk_kernel(tc, qT, k_words, k_scales, ts, kb, offs, o
             bank = psum.tile([P, hi - lo, P], F32, name="turned_tile%d_%d" % (s, lo), tag=tag)
             for t in range(lo, hi):
                 nc.tensor.transpose(bank[:, t - lo, :], yT[s][:, t, :], ident[:])
-            empty(y[s // 2][:, lo:hi, (s % 2) * P : (s % 2 + 1) * P], bank[:], on_vector)
+            dst = y[s // 2][:, lo:hi, (s % 2) * P : (s % 2 + 1) * P]
+            if s < 2:
+                empty(dst, bank[:], on_vector)
+            else:
+                nc.scalar.activation(dst, bank[:], SIGMOID)
 
         def store(h, lo, hi):
             nc.sync.dma_start(out_rows[:, lo:hi, h * HALF : (h + 1) * HALF], y[h][:, lo:hi, :])
@@ -177,18 +183,18 @@ def tile_attend_plq_sigts_topk_kernel(tc, qT, k_words, k_scales, ts, kb, offs, o
         def store_words(lo, hi):
             nc.sync.dma_start(out_words[:, lo:hi], y_codes[:, lo:hi].bitcast(I32))
 
-        turn_tile(0, 0, 2, "turn0", True)
+        turn_tile(0, 0, 2, "early0", True)
         store_tile(0, 0, 2)
-        turn_tile(1, 0, 2, "turn1", True)
+        turn_tile(1, 0, 2, "early1", False)
         store_tile(1, 0, 2)
-        turn(0, 2, 3, "early0", True)
-        turn(0, 3, 4, "early1", False)
+        turn(0, 2, 3, "early2", True)
+        turn(0, 3, 4, "early3", False)
         store(0, 2, 4)
-        turn_tile(2, 0, 2, "late0", False)
-        turn_tile(2, 2, 4, "late1", False)
-        turn_tile(3, 0, 2, "whole0", False)
+        turn_tile(2, 0, 2, "late3", False)
+        turn_tile(2, 2, 4, "early0", False)
+        turn_tile(3, 0, 2, "late0", False)
         store(1, 0, 2)
-        turn_tile(3, 2, 4, "whole1", False)
+        turn_tile(3, 2, 4, "late1", False)
         store(1, 2, 4)
         weave(0, 0, HALF, "v")
         weave(1, 0, P, "v")

@@ -81,16 +81,19 @@ def tile_attend_plq_sigts_topk_kernel(tc, qT, k_words, k_scales, ts, kb, offs, o
             src = src.rearrange("p t (c i) -> p c t i", i=4)
             if engine == "v":
                 nc.vector.tensor_copy(dst, src)
+            elif engine == "g":
+                nc.gpsimd.tensor_scalar(dst, src, 1.0, 0.0, MULT, ADD)
             else:
                 nc.scalar.copy(dst, src)
 
-        def quantize_queries(raw, engine, lo, hi):
+        def quantize_queries(raw, shares, lo, hi):
             q_bf = keep.tile([P, (hi - lo) * PACK], BF16, name="q_bf%d" % lo, align_bytes=64)
-            interleave(engine, q_bf[:], raw[:])
+            for engine, a, b in shares:
+                interleave(engine, q_bf[:, a * PACK : b * PACK], raw[:, :, a:b])
             nc.vector.quantize_mx(out=q_codes[:, lo:hi].bitcast(FP8X4), scales=q_sc[:, lo:hi], in_=q_bf[:])
 
         k_sc = keep.tile([P, SLOTS], U8, name="k_sc", align_bytes=64)
-        quantize_queries(q_early, "v", 0, HALF)
+        quantize_queries(q_early, (("v", 0, 160), ("g", 160, HALF)), 0, HALF)
         nc.vector.tensor_copy(k_sc[:], scale_pool[:].indirect(offsets[:]))
         k_g = []
         for h in range(2):
@@ -98,7 +101,7 @@ def tile_attend_plq_sigts_topk_kernel(tc, qT, k_words, k_scales, ts, kb, offs, o
             nc.vector.tensor_copy(words[:], word_pool[:].indirect(offsets[:, 16 * h : 16 * (h + 1)]))
             k_g.append(words)
         for n in range(2):
-            quantize_queries(q_late[n], "s", HALF + n * P, HALF + (n + 1) * P)
+            quantize_queries(q_late[n], (("s", 0, P),), HALF + n * P, HALF + (n + 1) * P)
 
         y_codes = keep.tile([P, SLOTS], U32, name="y_codes", align_bytes=64)
         y_sc = keep.tile([P, SLOTS], U8, name="y_sc", align_bytes=64)

@@ -62,9 +62,7 @@ def tile_attend_plq_sigts_topk_kernel(tc, qT, k_words, k_scales, ts, kb, offs, o
         for n in range(2):
             nc.sync.dma_start(q_late[n][:], q_rows[:, :, HALF + n * P : HALF + (n + 1) * P])
 
-        after_late = keep.tile([P, TILES * NQ + 2 * TILES], F32, name="after_late", tag="q_late1")
-        col = after_late[:, TILES * NQ :].rearrange("p (n s) -> p n s", n=2)
-        yT = [after_late[:, s * NQ : (s + 1) * NQ].rearrange("p (t m) -> p t m", t=PACK) for s in range(TILES)]
+        col = keep.tile([P, 2, TILES], F32, name="col")
         for n, pool in enumerate((ts_pool, kb_pool)):
             row = keep.tile([P, SLOTS], F32, name="rows%d" % n)
             nc.scalar.activation(row[:], pool[:].indirect(offsets[:]), COPY)
@@ -87,7 +85,7 @@ def tile_attend_plq_sigts_topk_kernel(tc, qT, k_words, k_scales, ts, kb, offs, o
                 nc.scalar.copy(dst, src)
 
         def quantize_queries(raw, shares, lo, hi):
-            q_bf = keep.tile([P, (hi - lo) * PACK], BF16, name="q_bf%d" % lo, align_bytes=64)
+            q_bf = keep.tile([P, (hi - lo) * PACK], BF16, name="q_bf%d" % lo, tag="q_bf%d" % lo, align_bytes=64)
             for engine, a, b in shares:
                 interleave(engine, q_bf[:, a * PACK : b * PACK], raw[:, :, a:b])
             nc.vector.quantize_mx(out=q_codes[:, lo:hi].bitcast(FP8X4), scales=q_sc[:, lo:hi], in_=q_bf[:])
@@ -100,8 +98,10 @@ def tile_attend_plq_sigts_topk_kernel(tc, qT, k_words, k_scales, ts, kb, offs, o
             words = keep.tile([P, HALF], U32, name="k_g%d" % h, align_bytes=64)
             nc.vector.tensor_copy(words[:], word_pool[:].indirect(offsets[:, 16 * h : 16 * (h + 1)]))
             k_g.append(words)
-        for n in range(2):
-            quantize_queries(q_late[n], (("s", 0, P),), HALF + n * P, HALF + (n + 1) * P)
+        quantize_queries(q_late[0], (("s", 0, P),), HALF, HALF + P)
+        quantize_queries(q_late[1], (("v", 0, P),), HALF + P, NQ)
+        yT = [keep.tile([P, PACK, P], F32, name="yT%d" % s) for s in range(TILES - 1)]
+        yT.append(keep.tile([P, PACK, P], F32, name="yT_last", tag="q_bf%d" % (HALF + P), align_bytes=64))
 
         y_codes = keep.tile([P, SLOTS], U32, name="y_codes", align_bytes=64)
         y_sc = keep.tile([P, SLOTS], U8, name="y_sc", align_bytes=64)
@@ -127,7 +127,7 @@ def tile_attend_plq_sigts_topk_kernel(tc, qT, k_words, k_scales, ts, kb, offs, o
         def weigh(s, lo, hi):
             dst = yT[s][:, :, lo // PACK : hi // PACK]
             src = bank_of(s, lo, hi).rearrange("p (m t) -> p t m", t=PACK)
-            if s < 2:
+            if s < TILES - 1:
                 nc.scalar.activation(dst, src, SIGMOID, bias=col[:, 1, s : s + 1], scale=col[:, 0, s : s + 1])
             else:
                 nc.vector.tensor_scalar(dst, src, col[:, 0, s : s + 1], col[:, 1, s : s + 1], MULT, ADD)
@@ -164,7 +164,7 @@ def tile_attend_plq_sigts_topk_kernel(tc, qT, k_words, k_scales, ts, kb, offs, o
             for t in range(lo, hi):
                 nc.tensor.transpose(bank[:, t - lo, :], yT[s][:, t, :], ident[:])
             dst = y[s // 2][:, lo:hi, (s % 2) * P : (s % 2 + 1) * P]
-            if s < 2:
+            if s < TILES - 1:
                 empty(dst, bank[:], on_vector)
             else:
                 nc.scalar.activation(dst, bank[:], SIGMOID)
@@ -193,7 +193,7 @@ def tile_attend_plq_sigts_topk_kernel(tc, qT, k_words, k_scales, ts, kb, offs, o
         turn(0, 2, 3, "early2", True)
         turn(0, 3, 4, "early3", False)
         store(0, 2, 4)
-        turn_tile(2, 0, 2, "late3", False)
+        turn_tile(2, 0, 2, "late3", True)
         turn_tile(2, 2, 4, "early0", False)
         turn_tile(3, 0, 2, "late0", False)
         store(1, 0, 2)

@@ -32,7 +32,7 @@ def tile_attend_plq_sigts_topk_kernel(tc, qT, k_words, k_scales, ts, kb, offs, o
 
         offsets = keep.tile([P, SLOTS // 16], U16, name="offsets")
         ts_pool = keep.tile([P, TOKENS], F32, name="ts_pool")
-        kb_pool = keep.tile([P, TOKENS], F32, name="kb_pool")
+        kb_pool = keep.tile([P, TOKENS], F32, name="kb_pool", tag="kb_pool")
         scale_pool = keep.tile([P, TOKENS], U8, name="scale_pool", align_bytes=64)
         word_pool = keep.tile([P, TOKENS], U32, name="word_pool", align_bytes=64)
         q_early = keep.tile([P, PACK, HALF], F32, name="q_early")
@@ -40,9 +40,9 @@ def tile_attend_plq_sigts_topk_kernel(tc, qT, k_words, k_scales, ts, kb, offs, o
 
         q_rows = qT[0].rearrange("(p j) c -> p j c", j=PACK)
         nc.sync.dma_start(ts_pool[P - 1 : P, :], ts[0:1, :])
-        nc.sync.dma_start(kb_pool[P - 1 : P, :], kb[0:1, :])
         nc.sync.dma_start(offsets[:], offs)
         nc.sync.dma_start(q_early[:], q_rows[:, :, 0:HALF])
+        nc.sync.dma_start(kb_pool[P - 1 : P, :], kb[0:1, :])
 
         warm = keep.tile([P, 1], F32, name="warm")
         nc.vector.memset(warm[:], 0.0)
@@ -62,7 +62,7 @@ def tile_attend_plq_sigts_topk_kernel(tc, qT, k_words, k_scales, ts, kb, offs, o
         for n in range(2):
             nc.sync.dma_start(q_late[n][:], q_rows[:, :, HALF + n * P : HALF + (n + 1) * P])
 
-        col = keep.tile([P, 2, TILES], F32, name="col")
+        col = keep.tile([P, 2, TILES], F32, name="col", tag="kb_pool")
         for n, pool in enumerate((ts_pool, kb_pool)):
             row = keep.tile([P, SLOTS], F32, name="rows%d" % n)
             nc.scalar.activation(row[:], pool[:].indirect(offsets[:]), COPY)
@@ -132,13 +132,9 @@ def tile_attend_plq_sigts_topk_kernel(tc, qT, k_words, k_scales, ts, kb, offs, o
             else:
                 nc.vector.tensor_scalar(dst, src, col[:, 0, s : s + 1], col[:, 1, s : s + 1], MULT, ADD)
 
-        for s in range(TILES):
-            product(s, 0, HALF)
-        for lo in (HALF, HALF + P):
-            for s in range(2):
-                product(s, lo, lo + P)
-        for s in range(2, TILES):
-            product(s, HALF, NQ)
+        for lo in (0, HALF):
+            for s in range(TILES):
+                product(s, lo, lo + HALF)
         for lo in (0, HALF):
             for s in range(TILES):
                 weigh(s, lo, lo + HALF)

@@ -132,9 +132,13 @@ def tile_attend_plq_sigts_topk_kernel(tc, qT, k_words, k_scales, ts, kb, offs, o
             else:
                 nc.vector.tensor_scalar(dst, src, col[:, 0, s : s + 1], col[:, 1, s : s + 1], MULT, ADD)
 
-        for lo in (0, HALF):
-            for s in range(TILES):
-                product(s, lo, lo + HALF)
+        for s in range(TILES):
+            product(s, 0, HALF)
+        for lo in (HALF, HALF + P):
+            for s in range(2):
+                product(s, lo, lo + P)
+        for s in range(2, TILES):
+            product(s, HALF, NQ)
         for lo in (0, HALF):
             for s in range(TILES):
                 weigh(s, lo, lo + HALF)

from contextlib import ExitStack

import concourse.mybir as mybir
from concourse.masks import make_identity

F32 = mybir.dt.float32
BF16 = mybir.dt.bfloat16
I32 = mybir.dt.int32
U32 = mybir.dt.uint32
U16 = mybir.dt.uint16
U8 = mybir.dt.uint8
FP8X4 = mybir.dt.float8_e4m3fn_x4
SIGMOID = mybir.ActivationFunctionType.Sigmoid
COPY = mybir.ActivationFunctionType.Copy
MULT = mybir.AluOpType.mult
ADD = mybir.AluOpType.add

P = 128
PACK = 4
D, NQ, SLOTS, TOKENS = 512, 512, 512, 2048
TILES = SLOTS // P
HALF = 256
FLOPS = 2 * D * NQ * SLOTS
BYTES = 4 * D * NQ + 4 * P * TOKENS + 16 * TOKENS + 2 * 4 * TOKENS + 2 * P * 32 + 4 * NQ * SLOTS + NQ * SLOTS + 16 * SLOTS


def tile_attend_plq_sigts_topk_kernel(tc, qT, k_words, k_scales, ts, kb, offs, out_0, out_1, out_2):
    nc = tc.nc
    with ExitStack() as ctx:
        keep = ctx.enter_context(tc.tile_pool(name="keep", bufs=1))
        psum = ctx.enter_context(tc.psum_pool(name="psum", bufs=1))

        offsets = keep.tile([P, SLOTS // 16], U16, name="offsets")
        ts_pool = keep.tile([P, TOKENS], F32, name="ts_pool")
        kb_pool = keep.tile([P, TOKENS], F32, name="kb_pool", tag="kb_pool")
        scale_pool = keep.tile([P, TOKENS], U8, name="scale_pool", align_bytes=64)
        word_pool = keep.tile([P, TOKENS], U32, name="word_pool", align_bytes=64)
        q_early = keep.tile([P, PACK, HALF], F32, name="q_early")
        q_late = [keep.tile([P, PACK, P], F32, name="q_late%d" % n, tag="q_late%d" % n) for n in range(2)]

        q_rows = qT[0].rearrange("(p j) c -> p j c", j=PACK)
        nc.sync.dma_start(ts_pool[P - 1 : P, :], ts[0:1, :])
        nc.sync.dma_start(offsets[:], offs)
        nc.sync.dma_start(q_early[:], q_rows[:, :, 0:HALF])
        nc.sync.dma_start(kb_pool[P - 1 : P, :], kb[0:1, :])

        warm = keep.tile([P, 1], F32, name="warm")
        nc.vector.memset(warm[:], 0.0)
        nc.scalar.activation(warm[:], warm[:], SIGMOID)

        nc.gpsimd.memset(scale_pool[:].bitcast(I32), 0)
        for pool in (ts_pool, kb_pool):
            nc.vector.memset(pool[0 : P - 1, 0:511], 0.0)
            nc.vector.memset(pool[0 : P - 1, 511:1024], 0.0)
            nc.gpsimd.memset(pool[0 : P - 1, 1024:TOKENS], 0.0)
        ident = keep.tile([P, P], F32, name="ident")
        make_identity(nc, ident[:])

        for r in range(4):
            nc.sync.dma_start(scale_pool[r:P:32, :].bitcast(I32), k_scales[0][r:16:4, :].bitcast(I32))
        nc.sync.dma_start(word_pool[:].bitcast(I32), k_words[0].rearrange("p n t -> p (n t)").bitcast(I32))
        for n in range(2):
            nc.sync.dma_start(q_late[n][:], q_rows[:, :, HALF + n * P : HALF + (n + 1) * P])

        col = keep.tile([P, 2, TILES], F32, name="col", tag="kb_pool")
        for n, pool in enumerate((ts_pool, kb_pool)):
            row = keep.tile([P, SLOTS], F32, name="rows%d" % n)
            nc.scalar.activation(row[:], pool[:].indirect(offsets[:]), COPY)
            bank = psum.tile([P, TILES, P], F32, name="cols%d" % n, tag="late%d" % (2 + n))
            for s in range(TILES):
                nc.tensor.transpose(bank[:, s, :], row[:, s * P : (s + 1) * P], ident[:])
            nc.scalar.copy(col[:, n, :], bank[:, :, P - 1])

        q_codes = keep.tile([P, NQ], U32, name="q_codes", align_bytes=64)
        q_sc = keep.tile([P, NQ], U8, name="q_sc", align_bytes=64)

        def interleave(engine, dst, src):
            dst = dst.rearrange("p (c i t) -> p c t i", i=4, t=PACK)
            src = src.rearrange("p t (c i) -> p c t i", i=4)
            if engine == "v":
                nc.vector.tensor_copy(dst, src)
            elif engine == "g":
                nc.gpsimd.tensor_scalar(dst, src, 1.0, 0.0, MULT, ADD)
            else:
                nc.scalar.copy(dst, src)

        def quantize_queries(raw, shares, lo, hi):
            q_bf = keep.tile([P, (hi - lo) * PACK], BF16, name="q_bf%d" % lo, tag="q_bf%d" % lo, align_bytes=64)
            for engine, a, b in shares:
                interleave(engine, q_bf[:, a * PACK : b * PACK], raw[:, :, a:b])
            nc.vector.quantize_mx(out=q_codes[:, lo:hi].bitcast(FP8X4), scales=q_sc[:, lo:hi], in_=q_bf[:])

        k_sc = keep.tile([P, SLOTS], U8, name="k_sc", align_bytes=64)
        quantize_queries(q_early, (("v", 0, 160), ("g", 160, HALF)), 0, HALF)
        nc.vector.tensor_copy(k_sc[:], scale_pool[:].indirect(offsets[:]))
        k_g = []
        for h in range(2):
            words = keep.tile([P, HALF], U32, name="k_g%d" % h, align_bytes=64)
            nc.vector.tensor_copy(words[:], word_pool[:].indirect(offsets[:, 16 * h : 16 * (h + 1)]))
            k_g.append(words)
        quantize_queries(q_late[0], (("s", 0, P),), HALF, HALF + P)
        quantize_queries(q_late[1], (("v", 0, P),), HALF + P, NQ)
        yT = [keep.tile([P, PACK, P], F32, name="yT%d" % s) for s in range(TILES - 1)]
        yT.append(keep.tile([P, PACK, P], F32, name="yT_last", tag="q_bf%d" % (HALF + P), align_bytes=64))

        y_codes = keep.tile([P, SLOTS], U32, name="y_codes", align_bytes=64)
        y_sc = keep.tile([P, SLOTS], U8, name="y_sc", align_bytes=64)
        out_rows = out_0.rearrange("(p t) i -> p t i", t=PACK)
        out_words = out_1[0].rearrange("p i u -> p (i u)").bitcast(I32)
        early = [psum.tile([P, HALF], F32, name="early%d" % s, tag="early%d" % s) for s in range(TILES)]
        late = [psum.tile([P, HALF], F32, name="late%d" % s, tag="late%d" % s) for s in range(TILES)]

        def bank_of(s, lo, hi):
            return early[s][:, lo:hi] if lo < HALF else late[s][:, lo - HALF : hi - HALF]

        def product(s, lo, hi):
            nc.tensor.matmul_mx(
                out=bank_of(s, lo, hi),
                lhsT=k_g[s // 2][:, (s % 2) * P : (s % 2 + 1) * P].bitcast(FP8X4),
                lhsT_scale=k_sc[:, s * P : (s + 1) * P],
                rhs=q_codes[:, lo:hi].bitcast(FP8X4),
                rhs_scale=q_sc[:, lo:hi],
                start=True,
                stop=True,
            )

        def weigh(s, lo, hi):
            dst = yT[s][:, :, lo // PACK : hi // PACK]
            src = bank_of(s, lo, hi).rearrange("p (m t) -> p t m", t=PACK)
            if s < TILES - 1:
                nc.scalar.activation(dst, src, SIGMOID, bias=col[:, 1, s : s + 1], scale=col[:, 0, s : s + 1])
            else:
                nc.vector.tensor_scalar(dst, src, col[:, 0, s : s + 1], col[:, 1, s : s + 1], MULT, ADD)

        for s in range(TILES):
            product(s, 0, HALF)
        for lo in (HALF, HALF + P):
            for s in range(2):
                product(s, lo, lo + P)
        for s in range(2, TILES):
            product(s, HALF, NQ)
        for lo in (0, HALF):
            for s in range(TILES):
                weigh(s, lo, lo + HALF)

        y = [keep.tile([P, PACK, HALF], F32, name="y%d" % h) for h in range(2)]
        y_bf = [keep.tile([P, HALF * PACK], BF16, name="y_bf%d" % h, align_bytes=64) for h in range(2)]

        def empty(dst, src, on_vector):
            if on_vector:
                nc.vector.tensor_copy(dst, src)
            else:
                nc.scalar.copy(dst, src)

        def turn(h, lo, hi, tag, on_vector):
            bank = psum.tile([P, hi - lo, 2, P], F32, name="turned%d_%d" % (h, lo), tag=tag)
            for t in range(lo, hi):
                for s in range(2):
                    nc.tensor.transpose(bank[:, t - lo, s, :], yT[2 * h + s][:, t, :], ident[:])
            empty(y[h][:, lo:hi, :], bank[:].rearrange("p u s i -> p u (s i)"), on_vector)

        def turn_tile(s, lo, hi, tag, on_vector):
            bank = psum.tile([P, hi - lo, P], F32, name="turned_tile%d_%d" % (s, lo), tag=tag)
            for t in range(lo, hi):
                nc.tensor.transpose(bank[:, t - lo, :], yT[s][:, t, :], ident[:])
            dst = y[s // 2][:, lo:hi, (s % 2) * P : (s % 2 + 1) * P]
            if s < TILES - 1:
                empty(dst, bank[:], on_vector)
            else:
                nc.scalar.activation(dst, bank[:], SIGMOID)

        def store(h, lo, hi):
            nc.sync.dma_start(out_rows[:, lo:hi, h * HALF : (h + 1) * HALF], y[h][:, lo:hi, :])

        def store_tile(s, lo, hi):
            nc.sync.dma_start(out_rows[:, lo:hi, s * P : (s + 1) * P], y[s // 2][:, lo:hi, (s % 2) * P : (s % 2 + 1) * P])

        def weave(h, lo, hi, engine):
            interleave(engine, y_bf[h][:, lo * PACK : hi * PACK], y[h][:, :, lo:hi])

        def quantize(lo, hi):
            h = lo // HALF
            src = y_bf[h][:, (lo - h * HALF) * PACK : (hi - h * HALF) * PACK]
            nc.vector.quantize_mx(out=y_codes[:, lo:hi].bitcast(FP8X4), scales=y_sc[:, lo:hi], in_=src)

        def store_words(lo, hi):
            nc.sync.dma_start(out_words[:, lo:hi], y_codes[:, lo:hi].bitcast(I32))

        turn_tile(0, 0, 2, "early0", True)
        store_tile(0, 0, 2)
        turn_tile(1, 0, 2, "early1", False)
        store_tile(1, 0, 2)
        turn(0, 2, 3, "early2", True)
        turn(0, 3, 4, "early3", False)
        store(0, 2, 4)
        turn_tile(2, 0, 2, "late3", True)
        turn_tile(2, 2, 4, "early0", False)
        turn_tile(3, 0, 2, "late0", False)
        store(1, 0, 2)
        turn_tile(3, 2, 4, "late1", False)
        store(1, 2, 4)
        weave(0, 0, HALF, "v")
        weave(1, 0, P, "v")
        quantize(0, HALF)
        quantize(HALF, 3 * P)
        store_words(0, 3 * P)
        weave(1, P, P + 32, "v")
        weave(1, P + 32, HALF, "s")
        quantize(3 * P, SLOTS)
        store_words(3 * P, SLOTS)
        for quad in range(4):
            queue = nc.scalar if quad % 2 == 0 else nc.sync
            queue.dma_start(
                out_2[0][4 * quad : 4 * quad + 4, :].bitcast(I32),
                y_sc[32 * quad : 32 * quad + 4, :].bitcast(I32),
            )
